import numpy as np
import ml_dtypes


def mxq(x, axis, fmt="e4m3"):
    dtype, down = {"e4m3": (ml_dtypes.float8_e4m3fn, 7), "e5m2": (ml_dtypes.float8_e5m2, 14)}[fmt]
    v = np.moveaxis(np.asarray(x, np.float32).astype(ml_dtypes.bfloat16).astype(np.float64), axis, -1)
    blocks = v.reshape(v.shape[:-1] + (-1, 32))
    amax = np.abs(blocks).max(-1, keepdims=True)
    byte = np.maximum(np.where(amax > 0, np.frexp(amax)[1] - 1 + 127, 0) - down, 1)
    scale = np.exp2(byte - 127.0)
    codes = (blocks / scale).astype(np.float32).astype(dtype).astype(np.float64)
    return np.moveaxis((codes * scale).reshape(v.shape), -1, axis)


WIDE = False


def mx_kscale(k):
    if not WIDE:
        return np.ones(k)
    levels = np.array([10, -10, 5, -5, 0])
    if k % 512:
        return np.exp2(np.random.permutation(np.resize(levels, k // 32))).repeat(32)
    a = np.empty((k // 512, 16))
    for p in range(k // 512):
        a[p, :8] = np.random.permutation(np.resize(levels, 8))
        for g in range(8):
            far = levels[np.abs(levels - a[p, g]) >= 10]
            a[p, g + 8] = far[np.random.randint(len(far))]
    return np.exp2(a.ravel()).repeat(32)


def f64(x):
    return np.asarray(x).astype(np.float64)


def striped(idx):
    return np.tile(np.asarray(idx).reshape(-1, 16).T, (8, 1)).astype(np.uint16)


def unstriped(offs):
    return offs[:16].T.reshape(-1).astype(np.int64)


E2M1 = np.array([0.0, 0.5, 1.0, 1.5, 2.0, 3.0, 4.0, 6.0, -0.0, -0.5, -1.0, -1.5, -2.0, -3.0, -4.0, -6.0])


def pack_weight(w, fmt):
    k, n = w.shape
    w = f64(np.asarray(w, np.float32).astype(ml_dtypes.bfloat16)).reshape(k // 32, 32, n)
    amax = np.abs(w).max(1)
    if fmt == "e4m3":
        byte = np.frexp(amax)[1] - 1 + 127 - 7
    else:
        mant, ex = np.frexp(amax / 6.0)
        byte = np.where(mant > 0.5, ex, ex - 1) + 127
    byte = np.clip(np.where(amax > 0, byte, 1), 1, 254)
    scaled = (w * np.exp2(127.0 - byte)[:, None, :]).reshape(k, n).astype(np.float32)
    by_word = np.ascontiguousarray(scaled.reshape(k // 512, 128, 4, n).transpose(0, 1, 3, 2))
    if fmt == "e4m3":
        words = by_word.astype(ml_dtypes.float8_e4m3fn).view(np.uint8)
    else:
        c = by_word.astype(ml_dtypes.float4_e2m1fn).view(np.uint8) & 0xF
        words = (c[..., 0::2] | (c[..., 1::2] << 4)).reshape(k // 512, 128, 2 * n)
    return np.ascontiguousarray(words), np.ascontiguousarray(byte.astype(np.uint8).reshape(k // 512, 16, n))


def unpack_weight(words, scales, fmt):
    g, _, n = scales.shape
    words = np.ascontiguousarray(words).reshape(g, 128, n, -1)
    if fmt == "e4m3":
        vals = words.view(ml_dtypes.float8_e4m3fn).astype(np.float64)
    else:
        nib = np.empty((g, 128, n, 4), np.uint8)
        nib[..., 0::2] = words & 0xF
        nib[..., 1::2] = words >> 4
        vals = E2M1[nib]
    vals = vals * np.repeat(np.exp2(scales.astype(np.float64) - 127.0), 8, axis=1)[..., None]
    return vals.transpose(0, 1, 3, 2).reshape(g * 512, n)


def sigmoid(v):
    return 1.0 / (1.0 + np.exp(-v))


def bf(x):
    return np.asarray(x, np.float32).astype(ml_dtypes.bfloat16)


def planes(Y):
    r, m = Y.shape
    b = f64(bf(Y)).reshape(r // 32, 32, m)
    amax = np.abs(b).max(1)
    byte = np.clip(np.where(amax > 0, np.frexp(amax)[1] - 1 + 127 - 7, 1), 1, 254)
    codes = (b * np.exp2(127.0 - byte)[:, None, :]).reshape(r, m).astype(np.float32).astype(ml_dtypes.float8_e4m3fn).view(np.uint8)
    words = codes.reshape(r // 512, 128, 4, m).transpose(0, 1, 3, 2)
    return np.ascontiguousarray(words), np.ascontiguousarray(byte.astype(np.uint8).reshape(r // 512, 16, m))


B, N, T, D, NQ = 1, 512, 2048, 1024, 512
DV = 512


def sgn(shape):
    return np.random.uniform(0.5, 2.0, shape) * np.where(np.random.standard_normal(shape) < 0, -1.0, 1.0)


def setup_inputs():
    n = np.random.standard_normal
    idx = np.random.permutation(T)[:B * N]
    s = mx_kscale(D)[:, None]
    u = mx_kscale(N)
    ut = np.ones(T)
    ut[idx] = u
    kp = pack_weight(n((D, T)) / s, "e2m1")
    return {
        "qT": (n((B, D, NQ)) * s * (1.00 / np.sqrt(D))).astype(np.float32),
        "k_words": np.ascontiguousarray(kp[0].reshape(1, 2, 128, T, 2).transpose(0, 2, 3, 1, 4)).reshape(1, 128, T, 4),
        "k_scales": kp[1],
        "vT": (n((DV, T)) / ut).astype(np.float32),
        "ts": np.tile(np.random.uniform(0.5, 2.0, 2048), (128, 1)).astype(np.float32),
        "kb": np.tile(n(2048), (128, 1)).astype(np.float32),
        "us": (sgn((B, N, 1)) * u[:, None]).astype(np.float32),
        "offs": striped(idx),
    }


def reference(qT, k_words, k_scales, vT, ts, kb, us, offs):
    idx = unstriped(offs)
    pick = lambda x, which: x[:, which].reshape(x.shape[0], B, -1).transpose(1, 0, 2)
    k = unpack_weight(k_words.reshape(1, 128, T, 2, 2).transpose(0, 3, 1, 2, 4).reshape(2, 128, 2 * T), k_scales, "e2m1")
    kg = pick(k, idx)
    qq = mxq(f64(qT), 1, "e4m3")
    a = kg.transpose(0, 2, 1) @ qq
    y = sigmoid(a * pick(f64(ts), idx)[:, :1, :].transpose(0, 2, 1) + pick(f64(kb), idx)[:, :1, :].transpose(0, 2, 1)) * f64(us)
    wq = mxq(y, 1, "e4m3")
    o = mxq(pick(f64(vT), idx).transpose(0, 2, 1), 1, "e4m3").transpose(0, 2, 1) @ wq
    Y = o[0]
    words, scales = planes(Y)
    return Y, words, scales

@@ -1,0 +1,217 @@
+from contextlib import ExitStack
+
+import concourse.mybir as mybir
+from concourse.masks import make_identity
+
+F32 = mybir.dt.float32
+BF16 = mybir.dt.bfloat16
+I32 = mybir.dt.int32
+U32 = mybir.dt.uint32
+U16 = mybir.dt.uint16
+U8 = mybir.dt.uint8
+FP8X4 = mybir.dt.float8_e4m3fn_x4
+FP4X4 = mybir.dt.float4_e2m1fn_x4
+ACT = mybir.ActivationFunctionType
+ALU = mybir.AluOpType
+
+P = 128
+N, T, D, NQ, DV = 512, 2048, 1024, 512, 512
+H = NQ // 2
+FLOPS = 2 * N * NQ * (D + DV)
+BYTES = 4 * D * NQ + 4 * P * T + 32 * T + 4 * DV * T + 8 * T + 4 * N + 2 * P * 32 + 4 * DV * NQ + DV * NQ + 16 * NQ
+
+
+def weave(copy, dst, src):
+    copy(dst.rearrange("p (c i) j -> p c j i", i=4), src.rearrange("p j (c i) -> p c j i", i=4))
+
+
+def quantize(nc, codes, scales, woven):
+    nc.vector.quantize_mx(out=codes.bitcast(FP8X4), scales=scales, in_=woven.rearrange("p w j -> p (w j)"))
+
+
+def tile_attend_plo_sigb_topk_kernel(tc, qT, k_words, k_scales, vT, ts, kb, us, offs, out_0, out_1, out_2):
+    nc = tc.nc
+    with ExitStack() as ctx:
+        keep = ctx.enter_context(tc.tile_pool(name="keep", bufs=1))
+        psum = ctx.enter_context(tc.psum_pool(name="psum", bufs=1))
+
+        offsets = keep.tile([P, N // 16], U16, name="offsets")
+        nc.sync.dma_start(offsets[:], offs)
+        ksw = keep.tile([P, T], U8, name="ksw")
+        nc.gpsimd.memset(ksw[:].bitcast(I32), 0)
+        tsw = keep.tile([P, T], F32, name="tsw")
+        nc.scalar.dma_start(tsw[127:128, :], ts[0:1, :])
+        nc.vector.memset(tsw[0:127, :].bitcast(I32), 0)
+        kbw = keep.tile([P, T], F32, name="big0")
+        nc.scalar.dma_start(kbw[127:128, :], kb[0:1, :])
+        nc.vector.memset(kbw[0:127, :].bitcast(I32), 0)
+        q_rows = [qT[0, 512 * o : 512 * (o + 1), :].rearrange("(p j) w -> p j w", j=4) for o in range(2)]
+        q_raw = [keep.tile([P, 4, NQ], F32, name=name) for name in ("q_raw0", "big1")]
+        nc.sync.dma_start(q_raw[0][:], q_rows[0])
+        for Q in range(4):
+            nc.sync.dma_start(
+                ksw[32 * Q : 32 * Q + 8, :].bitcast(I32), k_scales[:, 4 * Q : 4 * Q + 4, :].bitcast(I32)
+            )
+        nc.sync.dma_start(q_raw[1][:], q_rows[1])
+        kw = keep.tile([P, T], I32, name="big2")
+        nc.sync.dma_start(kw[:], k_words[0].rearrange("p t b -> p (t b)").bitcast(I32))
+        usr = keep.tile([P, N], F32, name="usr")
+        nc.scalar.dma_start(
+            usr[127:128, :].rearrange("p (t b i) -> p t b i", t=4, i=8),
+            us.rearrange("p (b t i) z -> p t b (i z)", t=4, i=8),
+        )
+        warm = keep.tile([P, 8], F32, name="warm")
+        nc.gpsimd.memset(warm[:, 0:1], 0.0)
+        nc.scalar.activation(warm[:, 1:2], warm[:, 0:1], ACT.Sigmoid)
+        nc.gpsimd.memset(usr[0:127, :], 0.0)
+        ident_f = keep.tile([P, P], F32, name="ident_f")
+        make_identity(nc, ident_f[:])
+        ident_b = keep.tile([P, P], BF16, name="ident_b")
+        make_identity(nc, ident_b[:])
+
+        def dealt_row(name, win):
+            g = keep.tile([P, N], F32, name=name)
+            nc.vector.tensor_copy(
+                g[:].bitcast(U32).rearrange("p (t b i) -> p b t i", t=4, i=8), win[:].bitcast(U32).indirect(offsets[:])
+            )
+            return g
+
+        tsg = dealt_row("tsg", tsw)
+        ksg = keep.tile([P, N], U8, name="ksg")
+        nc.vector.tensor_copy(ksg[:], ksw[:].indirect(offsets[:]))
+        ksd0 = keep.tile([P, N], U8, name="ksd0", align_bytes=64)
+        nc.vector.tensor_copy(
+            ksd0[:].bitcast(I32).rearrange("p (t b h) -> p t b h", t=4, h=2),
+            ksg[:].bitcast(I32).rearrange("p (b t h) -> p t b h", t=4, h=2),
+        )
+        ksd1 = keep.tile([P, N], U8, name="ksd1", align_bytes=64)
+        nc.sync.dma_start(ksd1[0:124, :].bitcast(I32), ksd0[4:128, :].bitcast(I32))
+        ksd = [ksd0, ksd1]
+        kbg = dealt_row("kbg", kbw)
+        dealt = [tsg, kbg, usr]
+        cols = keep.tile([P, 3, 8], F32, name="cols")
+
+        q_codes = [keep.tile([P, NQ], U32, name=f"q_codes{o}", align_bytes=64) for o in range(2)]
+        q_sc = [keep.tile([P, NQ], U8, name=f"q_sc{o}", align_bytes=64) for o in range(2)]
+        q_bf = [keep.tile([P, NQ, 4], BF16, name=f"q_bf{o}", align_bytes=64) for o in range(2)]
+        weave(nc.scalar.copy, q_bf[0][:], q_raw[0][:])
+        quantize(nc, q_codes[0][:], q_sc[0][:], q_bf[0][:])
+        QS = 384
+        weave(nc.scalar.copy, q_bf[1][:, 0:QS, :], q_raw[1][:, :, 0:QS])
+        weave(nc.vector.tensor_copy, q_bf[1][:, QS:NQ, :], q_raw[1][:, :, QS:NQ])
+        quantize(nc, q_codes[1][:], q_sc[1][:], q_bf[1][:])
+
+        for x, tag in ((2, "cols_ps"), (0, "vt_ps0"), (1, "vt_ps1")):
+            cols_ps = psum.tile([P, 4, P], F32, name=tag)
+            for t in range(4):
+                nc.tensor.transpose(cols_ps[:, t, :], dealt[x][:, P * t : P * (t + 1)], ident_f[:])
+            nc.scalar.copy(cols[:, x, 0:4], cols_ps[:, :, P - 1])
+
+        v_rows = vT.rearrange("(p j) t -> j p t", j=4)
+
+        def load_values(j):
+            t_ = keep.tile([P, T], F32, name=f"big{j % 3}")
+            nc.sync.dma_start(t_[:], v_rows[j])
+            return t_
+
+        v_raw = [load_values(0), load_values(1)]
+
+        kg = keep.tile([P, N], U32, name="kg")
+        nc.vector.tensor_copy(kg[:], kw[:].bitcast(U32).indirect(offsets[:]))
+        k16 = [keep.tile([P, 2 * N], U8, name=f"k16_{o}", align_bytes=64) for o in range(2)]
+        for o in range(2):
+            nc.vector.tensor_copy(
+                k16[o][:].bitcast(U16).rearrange("p (t b i) -> p t b i", t=4, i=8),
+                kg[:].bitcast(U16).rearrange("p (b t i o) -> p o t b i", t=4, i=8, o=2)[:, o],
+            )
+
+        v_raw.append(load_values(2))
+
+        banks = [psum.tile([P, NQ], F32, name=f"bank{t}") for t in range(4)]
+        for o in range(2):
+            for t in range(4):
+                nc.tensor.matmul_mx(
+                    out=banks[t][:],
+                    lhsT=k16[o][:, 256 * t : 256 * (t + 1)].bitcast(FP4X4),
+                    lhsT_scale=ksd[o][:, P * t : P * (t + 1)],
+                    rhs=q_codes[o][:].bitcast(FP8X4),
+                    rhs_scale=q_sc[o][:],
+                    start=(o == 0),
+                    stop=(o == 1),
+                )
+
+        v_codes, v_sc = [], []
+
+        def values(j):
+            vg = keep.tile([P, 4, P], BF16, name=f"vg{j}")
+            nc.vector.tensor_copy(vg[:].rearrange("p t (b i) -> p b t i", i=8), v_raw[j][:].indirect(offsets[:]))
+            if j == 0:
+                v_raw.append(load_values(3))
+            vt_ps = psum.tile([P, 4, P], BF16, name=f"vt_ps{j % 2}")
+            for t in range(4):
+                nc.tensor.transpose(vt_ps[:, t, :], vg[:, t, :], ident_b[:])
+            v_bf = keep.tile([P, P, 4], BF16, name=f"v_bf{j}", align_bytes=64)
+            nc.scalar.copy(v_bf[:], vt_ps[:].rearrange("p t m -> p m t"))
+            codes = keep.tile([P, P], U32, name=f"v_codes{j}", align_bytes=64)
+            sc = keep.tile([P, P], U8, name=f"v_sc{j}", align_bytes=64)
+            quantize(nc, codes[:], sc[:], v_bf[:])
+            v_codes.append(codes)
+            v_sc.append(sc)
+
+        y_codes = keep.tile([P, NQ], U32, name="y_codes", align_bytes=64)
+        y_sc = keep.tile([P, NQ], U8, name="y_sc", align_bytes=64)
+        for h in range(2):
+            sg = keep.tile([P, 4, H], F32, name=f"sg{h}")
+            for t in range(4):
+                nc.scalar.activation(
+                    sg[:, t, :], banks[t][:, H * h : H * (h + 1)], ACT.Sigmoid,
+                    bias=cols[:, 1, t : t + 1], scale=cols[:, 0, t : t + 1],
+                )
+            y_bf = keep.tile([P, H, 4], BF16, name=f"y_bf{h}", align_bytes=64)
+            nc.vector.tensor_tensor(
+                y_bf[:].rearrange("p (c i) t -> p c t i", i=4),
+                sg[:].rearrange("p t (c i) -> p c t i", i=4),
+                cols[:, 2, 0:4].unsqueeze(1).unsqueeze(3).to_broadcast([P, H // 4, 4, 4]),
+                ALU.mult,
+            )
+            quantize(nc, y_codes[:, H * h : H * (h + 1)], y_sc[:, H * h : H * (h + 1)], y_bf[:])
+            values(h)
+        values(2)
+
+        res = keep.tile([P, 4, NQ], F32, name="res")
+        out_rows = out_0.rearrange("(p j) q -> j p q", j=4)
+        for j in range(3):
+            acc = psum.tile([P, NQ], F32, name=f"bank{j}")
+            nc.tensor.matmul_mx(
+                out=acc[:], lhsT=v_codes[j][:].bitcast(FP8X4), lhsT_scale=v_sc[j][:],
+                rhs=y_codes[:].bitcast(FP8X4), rhs_scale=y_sc[:], start=True, stop=True,
+            )
+            nc.scalar.copy(res[:, j, :], acc[:])
+            nc.sync.dma_start(out_rows[j], res[:, j, :])
+        values(3)
+        o_codes = keep.tile([P, NQ], I32, name="o_codes", align_bytes=64)
+        o_sc = keep.tile([P, NQ], U8, name="o_sc", align_bytes=64)
+        o_bf = keep.tile([P, NQ, 4], BF16, name="o_bf", align_bytes=64)
+        words = out_1[0].rearrange("p q u -> p (q u)").bitcast(I32)
+        copies = (nc.vector.tensor_copy, nc.scalar.copy)
+        for h in range(2):
+            acc = psum.tile([P, H], F32, name=("bank3", "cols_ps")[h])
+            cs = slice(H * h, H * (h + 1))
+            nc.tensor.matmul_mx(
+                out=acc[:], lhsT=v_codes[3][:].bitcast(FP8X4), lhsT_scale=v_sc[3][:],
+                rhs=y_codes[:, cs].bitcast(FP8X4), rhs_scale=y_sc[:, cs], start=True, stop=True,
+            )
+            copies[h](res[:, 3, cs], acc[:])
+        nc.sync.dma_start(out_rows[3], res[:, 3, :])
+        TV = 64
+        weave(nc.vector.tensor_copy, o_bf[:, 0:H, :], res[:, :, 0:H])
+        weave(nc.scalar.copy, o_bf[:, H + TV : NQ, :], res[:, :, H + TV : NQ])
+        quantize(nc, o_codes[:, 0:H], o_sc[:, 0:H], o_bf[:, 0:H, :])
+        nc.sync.dma_start(words[:, 0:H], o_codes[:, 0:H])
+        weave(nc.vector.tensor_copy, o_bf[:, H : H + TV, :], res[:, :, H : H + TV])
+        quantize(nc, o_codes[:, H:NQ], o_sc[:, H:NQ], o_bf[:, H:NQ, :])
+        nc.sync.dma_start(words[:, H:NQ], o_codes[:, H:NQ])
+        for Q in range(4):
+            (nc.scalar, nc.sync)[Q % 2].dma_start(
+                out_2[0, 4 * Q : 4 * Q + 4, :].bitcast(I32), o_sc[32 * Q : 32 * Q + 4, :].bitcast(I32)
+            )

@@ -37,84 +37,82 @@ def tile_attend_plo_sigb_topk_kernel(tc, qT, k_words, k_scales, vT, ts, kb, us, 
 
         offsets = keep.tile([P, N // 16], U16, name="offsets")
         nc.sync.dma_start(offsets[:], offs)
-        ksw = keep.tile([P, T], U8, name="ksw")
-        nc.gpsimd.memset(ksw[:].bitcast(I32), 0)
+        ksw = keep.tile([P, 2, T], U8, name="ksw")
+        nc.gpsimd.memset(ksw[:].rearrange("p o t -> p (o t)").bitcast(I32), 0)
         tsw = keep.tile([P, T], F32, name="tsw")
         nc.scalar.dma_start(tsw[127:128, :], ts[0:1, :])
         nc.vector.memset(tsw[0:127, :].bitcast(I32), 0)
-        kbw = keep.tile([P, T], F32, name="big0")
+        kbw = keep.tile([P, T], F32, name="kbw")
         nc.scalar.dma_start(kbw[127:128, :], kb[0:1, :])
         nc.vector.memset(kbw[0:127, :].bitcast(I32), 0)
         q_rows = [qT[0, 512 * o : 512 * (o + 1), :].rearrange("(p j) w -> p j w", j=4) for o in range(2)]
-        q_raw = [keep.tile([P, 4, NQ], F32, name=name) for name in ("q_raw0", "big1")]
-        nc.sync.dma_start(q_raw[0][:], q_rows[0])
+        q0_raw = [keep.tile([P, 4, H], F32, name=f"q0_raw{h}") for h in range(2)]
+        q1_raw = keep.tile([P, 4, NQ], F32, name="q1_raw")
+        for h in range(2):
+            nc.sync.dma_start(q0_raw[h][:], q_rows[0][:, :, H * h : H * (h + 1)])
+        kw = keep.tile([P, T], I32, name="kw")
+        kw_rows = k_words[0].rearrange("p t b -> p (t b)").bitcast(I32)
+        for h in range(2):
+            nc.sync.dma_start(kw[:, T // 2 * h : T // 2 * (h + 1)], kw_rows[:, T // 2 * h : T // 2 * (h + 1)])
         for Q in range(4):
             nc.sync.dma_start(
-                ksw[32 * Q : 32 * Q + 8, :].bitcast(I32), k_scales[:, 4 * Q : 4 * Q + 4, :].bitcast(I32)
+                ksw[32 * Q : 32 * Q + 4].bitcast(I32),
+                k_scales[:, 4 * Q : 4 * Q + 4, :].rearrange("o r t -> r o t").bitcast(I32),
             )
-        nc.sync.dma_start(q_raw[1][:], q_rows[1])
-        kw = keep.tile([P, T], I32, name="big2")
-        nc.sync.dma_start(kw[:], k_words[0].rearrange("p t b -> p (t b)").bitcast(I32))
-        usr = keep.tile([P, N], F32, name="usr")
+        usr = keep.tile([P, P], F32, name="usr")
         nc.scalar.dma_start(
-            usr[127:128, :].rearrange("p (t b i) -> p t b i", t=4, i=8),
-            us.rearrange("p (b t i) z -> p t b (i z)", t=4, i=8),
+            usr[124:128, :].rearrange("t (b i) -> t b i", i=8),
+            us[0].rearrange("(b t i) z -> t b (i z)", t=4, i=8),
         )
+        nc.sync.dma_start(q1_raw[:], q_rows[1])
+        v_rows = vT.rearrange("(p j) t -> j p t", j=4)
+
+        def load_values(j):
+            t_ = keep.tile([P, T], F32, name=f"v_raw{j}")
+            nc.sync.dma_start(t_[:], v_rows[j])
+            return t_
+
+        v_raw = [load_values(j) for j in range(4)]
         warm = keep.tile([P, 8], F32, name="warm")
         nc.gpsimd.memset(warm[:, 0:1], 0.0)
         nc.scalar.activation(warm[:, 1:2], warm[:, 0:1], ACT.Sigmoid)
-        nc.gpsimd.memset(usr[0:127, :], 0.0)
+        nc.gpsimd.memset(usr[0:124, :], 0.0)
         ident_f = keep.tile([P, P], F32, name="ident_f")
         make_identity(nc, ident_f[:])
         ident_b = keep.tile([P, P], BF16, name="ident_b")
-        make_identity(nc, ident_b[:])
+        nc.scalar.copy(ident_b[:], ident_f[:])
+        cols = keep.tile([P, 3, 8], F32, name="cols")
 
-        def dealt_row(name, win):
+        def columns(x, name, win, tag):
             g = keep.tile([P, N], F32, name=name)
             nc.vector.tensor_copy(
                 g[:].bitcast(U32).rearrange("p (t b i) -> p b t i", t=4, i=8), win[:].bitcast(U32).indirect(offsets[:])
             )
-            return g
-
-        tsg = dealt_row("tsg", tsw)
-        ksg = keep.tile([P, N], U8, name="ksg")
-        nc.vector.tensor_copy(ksg[:], ksw[:].indirect(offsets[:]))
-        ksd0 = keep.tile([P, N], U8, name="ksd0", align_bytes=64)
-        nc.vector.tensor_copy(
-            ksd0[:].bitcast(I32).rearrange("p (t b h) -> p t b h", t=4, h=2),
-            ksg[:].bitcast(I32).rearrange("p (b t h) -> p t b h", t=4, h=2),
-        )
-        ksd1 = keep.tile([P, N], U8, name="ksd1", align_bytes=64)
-        nc.sync.dma_start(ksd1[0:124, :].bitcast(I32), ksd0[4:128, :].bitcast(I32))
-        ksd = [ksd0, ksd1]
-        kbg = dealt_row("kbg", kbw)
-        dealt = [tsg, kbg, usr]
-        cols = keep.tile([P, 3, 8], F32, name="cols")
+            cols_ps = psum.tile([P, 4, P], F32, name=tag)
+            for t in range(4):
+                nc.tensor.transpose(cols_ps[:, t, :], g[:, P * t : P * (t + 1)], ident_f[:])
+            nc.scalar.copy(cols[:, x, 0:4], cols_ps[:, :, P - 1])
 
         q_codes = [keep.tile([P, NQ], U32, name=f"q_codes{o}", align_bytes=64) for o in range(2)]
         q_sc = [keep.tile([P, NQ], U8, name=f"q_sc{o}", align_bytes=64) for o in range(2)]
         q_bf = [keep.tile([P, NQ, 4], BF16, name=f"q_bf{o}", align_bytes=64) for o in range(2)]
-        weave(nc.scalar.copy, q_bf[0][:], q_raw[0][:])
+        for h in range(2):
+            weave(nc.scalar.copy, q_bf[0][:, H * h : H * (h + 1), :], q0_raw[h][:])
+
+        columns(0, "tsg", tsw, "vt_ps0")
+        columns(1, "kbg", kbw, "vt_ps1")
         quantize(nc, q_codes[0][:], q_sc[0][:], q_bf[0][:])
-        QS = 384
-        weave(nc.scalar.copy, q_bf[1][:, 0:QS, :], q_raw[1][:, :, 0:QS])
-        weave(nc.vector.tensor_copy, q_bf[1][:, QS:NQ, :], q_raw[1][:, :, QS:NQ])
-        quantize(nc, q_codes[1][:], q_sc[1][:], q_bf[1][:])
-
-        for x, tag in ((2, "cols_ps"), (0, "vt_ps0"), (1, "vt_ps1")):
-            cols_ps = psum.tile([P, 4, P], F32, name=tag)
-            for t in range(4):
-                nc.tensor.transpose(cols_ps[:, t, :], dealt[x][:, P * t : P * (t + 1)], ident_f[:])
-            nc.scalar.copy(cols[:, x, 0:4], cols_ps[:, :, P - 1])
-
-        v_rows = vT.rearrange("(p j) t -> j p t", j=4)
-
-        def load_values(j):
-            t_ = keep.tile([P, T], F32, name=f"big{j % 3}")
-            nc.sync.dma_start(t_[:], v_rows[j])
-            return t_
-
-        v_raw = [load_values(0), load_values(1)]
+        us_ps = psum.tile([P, P], F32, name="cols_ps")
+        nc.tensor.transpose(us_ps[:], usr[:], ident_f[:])
+        nc.scalar.copy(cols[:, 2, 0:4], us_ps[:, 124:128])
+        ksg = keep.tile([P, 2, N], U8, name="ksg")
+        for o in range(2):
+            nc.vector.tensor_copy(ksg[:, o, :], ksw[:, o, :].indirect(offsets[:]))
+        ksd = keep.tile([P, 2, N], U8, name="ksd", align_bytes=64)
+        nc.vector.tensor_copy(
+            ksd[:].bitcast(I32).rearrange("p o (t b h) -> p o t b h", t=4, h=2),
+            ksg[:].bitcast(I32).rearrange("p o (b t h) -> p o t b h", t=4, h=2),
+        )
 
         kg = keep.tile([P, N], U32, name="kg")
         nc.vector.tensor_copy(kg[:], kw[:].bitcast(U32).indirect(offsets[:]))
@@ -124,30 +122,32 @@ def tile_attend_plo_sigb_topk_kernel(tc, qT, k_words, k_scales, vT, ts, kb, us, 
                 k16[o][:].bitcast(U16).rearrange("p (t b i) -> p t b i", t=4, i=8),
                 kg[:].bitcast(U16).rearrange("p (b t i o) -> p o t b i", t=4, i=8, o=2)[:, o],
             )
-
-        v_raw.append(load_values(2))
-
         banks = [psum.tile([P, NQ], F32, name=f"bank{t}") for t in range(4)]
-        for o in range(2):
+
+        def scores(o):
             for t in range(4):
                 nc.tensor.matmul_mx(
                     out=banks[t][:],
                     lhsT=k16[o][:, 256 * t : 256 * (t + 1)].bitcast(FP4X4),
-                    lhsT_scale=ksd[o][:, P * t : P * (t + 1)],
+                    lhsT_scale=ksd[:, o, P * t : P * (t + 1)],
                     rhs=q_codes[o][:].bitcast(FP8X4),
                     rhs_scale=q_sc[o][:],
                     start=(o == 0),
                     stop=(o == 1),
                 )
 
+        scores(0)
+        QS = 512
+        weave(nc.scalar.copy, q_bf[1][:, 0:QS, :], q1_raw[:, :, 0:QS])
+        quantize(nc, q_codes[1][:], q_sc[1][:], q_bf[1][:])
+        scores(1)
+
         v_codes, v_sc = [], []
 
         def values(j):
-            vg = keep.tile([P, 4, P], BF16, name=f"vg{j}")
+            vg = keep.tile([P, 4, P], BF16, name=("vg0", "vg1", "sg1", "vg3")[j])
             nc.vector.tensor_copy(vg[:].rearrange("p t (b i) -> p b t i", i=8), v_raw[j][:].indirect(offsets[:]))
-            if j == 0:
-                v_raw.append(load_values(3))
-            vt_ps = psum.tile([P, 4, P], BF16, name=f"vt_ps{j % 2}")
+            vt_ps = psum.tile([P, 4, P], BF16, name=("bank3", "bank2", "vt_ps0", "vt_ps1")[j])
             for t in range(4):
                 nc.tensor.transpose(vt_ps[:, t, :], vg[:, t, :], ident_b[:])
             v_bf = keep.tile([P, P, 4], BF16, name=f"v_bf{j}", align_bytes=64)
@@ -175,13 +175,13 @@ def tile_attend_plo_sigb_topk_kernel(tc, qT, k_words, k_scales, vT, ts, kb, us, 
                 ALU.mult,
             )
             quantize(nc, y_codes[:, H * h : H * (h + 1)], y_sc[:, H * h : H * (h + 1)], y_bf[:])
-            values(h)
-        values(2)
+        for j in range(3):
+            values(j)
 
         res = keep.tile([P, 4, NQ], F32, name="res")
         out_rows = out_0.rearrange("(p j) q -> j p q", j=4)
         for j in range(3):
-            acc = psum.tile([P, NQ], F32, name=f"bank{j}")
+            acc = psum.tile([P, NQ], F32, name=("bank0", "bank1", "acc2")[j])
             nc.tensor.matmul_mx(
                 out=acc[:], lhsT=v_codes[j][:].bitcast(FP8X4), lhsT_scale=v_sc[j][:],
                 rhs=y_codes[:].bitcast(FP8X4), rhs_scale=y_sc[:], start=True, stop=True,

@@ -11,207 +11,240 @@ U16 = mybir.dt.uint16
 U8 = mybir.dt.uint8
 FP8X4 = mybir.dt.float8_e4m3fn_x4
 FP4X4 = mybir.dt.float4_e2m1fn_x4
-ACT = mybir.ActivationFunctionType
-ALU = mybir.AluOpType
+SIGMOID = mybir.ActivationFunctionType.Sigmoid
+COPY = mybir.ActivationFunctionType.Copy
+MULT = mybir.AluOpType.mult
 
 P = 128
+PLACES = 4
 N, T, D, NQ, DV = 512, 2048, 1024, 512, 512
-H = NQ // 2
+HALF = NQ // 2
+LAST = P - 1
+Q_SCALAR = 320
+OUT_SCALAR = 128
+
 FLOPS = 2 * N * NQ * (D + DV)
-BYTES = 4 * D * NQ + 4 * P * T + 32 * T + 4 * DV * T + 8 * T + 4 * N + 2 * P * 32 + 4 * DV * NQ + DV * NQ + 16 * NQ
+BYTES = 4 * D * NQ + 4 * P * T + 32 * T + 4 * DV * T + 8 * T + 4 * N + 2 * P * (N // 16) + 5 * DV * NQ + 16 * NQ
 
 
 def weave(copy, dst, src):
-    copy(dst.rearrange("p (c i) j -> p c j i", i=4), src.rearrange("p j (c i) -> p c j i", i=4))
+    copy(dst.rearrange("p (c i) t -> p c t i", i=4), src.rearrange("p t (c i) -> p c t i", i=4))
 
 
 def quantize(nc, codes, scales, woven):
-    nc.vector.quantize_mx(out=codes.bitcast(FP8X4), scales=scales, in_=woven.rearrange("p w j -> p (w j)"))
+    nc.vector.quantize_mx(out=codes.bitcast(FP8X4), scales=scales, in_=woven.rearrange("p w t -> p (w t)"))
 
 
 def tile_attend_plo_sigb_topk_kernel(tc, qT, k_words, k_scales, vT, ts, kb, us, offs, out_0, out_1, out_2):
     nc = tc.nc
     with ExitStack() as ctx:
-        keep = ctx.enter_context(tc.tile_pool(name="keep", bufs=1))
+        sbuf = ctx.enter_context(tc.tile_pool(name="sbuf", bufs=1))
         psum = ctx.enter_context(tc.psum_pool(name="psum", bufs=1))
 
-        offsets = keep.tile([P, N // 16], U16, name="offsets")
+        def tile(shape, dtype, name):
+            return sbuf.tile(shape, dtype, name=name, align_bytes=64)
+
+        offsets = tile([P, N // 16], U16, "offsets")
         nc.sync.dma_start(offsets[:], offs)
-        ksw = keep.tile([P, 2, T], U8, name="ksw")
-        nc.gpsimd.memset(ksw[:].rearrange("p o t -> p (o t)").bitcast(I32), 0)
-        tsw = keep.tile([P, T], F32, name="tsw")
-        nc.scalar.dma_start(tsw[127:128, :], ts[0:1, :])
-        nc.vector.memset(tsw[0:127, :].bitcast(I32), 0)
-        kbw = keep.tile([P, T], F32, name="kbw")
-        nc.scalar.dma_start(kbw[127:128, :], kb[0:1, :])
-        nc.vector.memset(kbw[0:127, :].bitcast(I32), 0)
-        q_rows = [qT[0, 512 * o : 512 * (o + 1), :].rearrange("(p j) w -> p j w", j=4) for o in range(2)]
-        q0_raw = [keep.tile([P, 4, H], F32, name=f"q0_raw{h}") for h in range(2)]
-        q1_raw = keep.tile([P, 4, NQ], F32, name="q1_raw")
-        for h in range(2):
-            nc.sync.dma_start(q0_raw[h][:], q_rows[0][:, :, H * h : H * (h + 1)])
-        kw = keep.tile([P, T], I32, name="kw")
-        kw_rows = k_words[0].rearrange("p t b -> p (t b)").bitcast(I32)
-        for h in range(2):
-            nc.sync.dma_start(kw[:, T // 2 * h : T // 2 * (h + 1)], kw_rows[:, T // 2 * h : T // 2 * (h + 1)])
+        ks_window = tile([P, T], U8, "ks_window")
+        nc.gpsimd.memset(ks_window[:].bitcast(I32), 0)
+        warm = tile([P, 2], F32, "warm")
+        nc.gpsimd.memset(warm[:, 0:1], 0.0)
+        ts_window = tile([P, T], F32, "ts_window")
+        nc.scalar.dma_start(ts_window[LAST:P, :], ts[0:1, :])
+        nc.vector.memset(ts_window[0:LAST, :].bitcast(I32), 0)
+        kb_window = tile([P, T], F32, "kb_window")
+        nc.gpsimd.memset(kb_window[0:LAST, :].bitcast(I32), 0)
+        nc.scalar.dma_start(kb_window[LAST:P, :], kb[0:1, :])
+        q_rows = qT[0].rearrange("(o p t) w -> o p t w", o=2, t=PLACES)
+        q_raw = [tile([P, PLACES, NQ], F32, f"q_raw{o}") for o in range(2)]
+        nc.sync.dma_start(q_raw[0][:], q_rows[0])
         for Q in range(4):
             nc.sync.dma_start(
-                ksw[32 * Q : 32 * Q + 4].bitcast(I32),
-                k_scales[:, 4 * Q : 4 * Q + 4, :].rearrange("o r t -> r o t").bitcast(I32),
+                ks_window[32 * Q : 32 * Q + 8, :].bitcast(I32), k_scales[:, 4 * Q : 4 * Q + 4, :].bitcast(I32)
             )
-        usr = keep.tile([P, P], F32, name="usr")
-        nc.scalar.dma_start(
-            usr[124:128, :].rearrange("t (b i) -> t b i", i=8),
-            us[0].rearrange("(b t i) z -> t b (i z)", t=4, i=8),
-        )
-        nc.sync.dma_start(q1_raw[:], q_rows[1])
-        v_rows = vT.rearrange("(p j) t -> j p t", j=4)
+        kw_window = tile([P, T], I32, "kw_window")
+        nc.sync.dma_start(kw_window[:], k_words[0].rearrange("p t b -> p (t b)").bitcast(I32))
+        us_cols = tile([P, PLACES], F32, "us_cols")
+        nc.sync.dma_start(us_cols[:], us[0].rearrange("(p t) z -> p (t z)", t=PLACES))
+        nc.sync.dma_start(q_raw[1][:], q_rows[1])
+        v_rows = vT.rearrange("(p j) t -> j p t", j=PLACES)
 
         def load_values(j):
-            t_ = keep.tile([P, T], F32, name=f"v_raw{j}")
-            nc.sync.dma_start(t_[:], v_rows[j])
-            return t_
+            window = tile([P, T], F32, f"v_window{j}")
+            nc.sync.dma_start(window[:], v_rows[j])
+            return window
 
-        v_raw = [load_values(j) for j in range(4)]
-        warm = keep.tile([P, 8], F32, name="warm")
-        nc.gpsimd.memset(warm[:, 0:1], 0.0)
-        nc.scalar.activation(warm[:, 1:2], warm[:, 0:1], ACT.Sigmoid)
-        nc.gpsimd.memset(usr[0:124, :], 0.0)
-        ident_f = keep.tile([P, P], F32, name="ident_f")
-        make_identity(nc, ident_f[:])
-        ident_b = keep.tile([P, P], BF16, name="ident_b")
-        nc.scalar.copy(ident_b[:], ident_f[:])
-        cols = keep.tile([P, 3, 8], F32, name="cols")
+        v_window = [load_values(0)]
+        nc.scalar.activation(warm[:, 1:2], warm[:, 0:1], SIGMOID)
+        identity = tile([P, P], F32, "identity")
+        make_identity(nc, identity[:])
 
-        def columns(x, name, win, tag):
-            g = keep.tile([P, N], F32, name=name)
-            nc.vector.tensor_copy(
-                g[:].bitcast(U32).rearrange("p (t b i) -> p b t i", t=4, i=8), win[:].bitcast(U32).indirect(offsets[:])
-            )
-            cols_ps = psum.tile([P, 4, P], F32, name=tag)
-            for t in range(4):
-                nc.tensor.transpose(cols_ps[:, t, :], g[:, P * t : P * (t + 1)], ident_f[:])
-            nc.scalar.copy(cols[:, x, 0:4], cols_ps[:, :, P - 1])
+        q_woven = [tile([P, NQ, PLACES], BF16, f"q_woven{o}") for o in range(2)]
+        weave(nc.scalar.copy, q_woven[0][:], q_raw[0][:])
 
-        q_codes = [keep.tile([P, NQ], U32, name=f"q_codes{o}", align_bytes=64) for o in range(2)]
-        q_sc = [keep.tile([P, NQ], U8, name=f"q_sc{o}", align_bytes=64) for o in range(2)]
-        q_bf = [keep.tile([P, NQ, 4], BF16, name=f"q_bf{o}", align_bytes=64) for o in range(2)]
-        for h in range(2):
-            weave(nc.scalar.copy, q_bf[0][:, H * h : H * (h + 1), :], q0_raw[h][:])
+        def token_columns(window, name, bank):
+            listed = tile([P, N], F32, name + "_listed")
+            nc.vector.tensor_copy(listed[:], window[:].indirect(offsets[:]))
+            turned = psum.tile([P, PLACES, P], F32, name=bank)
+            for t in range(PLACES):
+                nc.tensor.transpose(turned[:, t, :], listed[:, t:N:PLACES], identity[:])
+            columns = tile([P, PLACES], F32, name + "_cols")
+            nc.scalar.copy(columns[:], turned[:, :, LAST])
+            return columns
 
-        columns(0, "tsg", tsw, "vt_ps0")
-        columns(1, "kbg", kbw, "vt_ps1")
-        quantize(nc, q_codes[0][:], q_sc[0][:], q_bf[0][:])
-        us_ps = psum.tile([P, P], F32, name="cols_ps")
-        nc.tensor.transpose(us_ps[:], usr[:], ident_f[:])
-        nc.scalar.copy(cols[:, 2, 0:4], us_ps[:, 124:128])
-        ksg = keep.tile([P, 2, N], U8, name="ksg")
-        for o in range(2):
-            nc.vector.tensor_copy(ksg[:, o, :], ksw[:, o, :].indirect(offsets[:]))
-        ksd = keep.tile([P, 2, N], U8, name="ksd", align_bytes=64)
+        ts_cols = token_columns(ts_window, "ts", "turn0")
+        kb_cols = token_columns(kb_window, "kb", "turn1")
+
+        ks_listed = tile([P, N], U8, "ks_listed")
+        nc.vector.tensor_copy(ks_listed[:], ks_window[:].indirect(offsets[:]))
+        k_plane = [tile([P, N], U8, f"k_plane{o}") for o in range(2)]
         nc.vector.tensor_copy(
-            ksd[:].bitcast(I32).rearrange("p o (t b h) -> p o t b h", t=4, h=2),
-            ksg[:].bitcast(I32).rearrange("p o (b t h) -> p o t b h", t=4, h=2),
+            k_plane[0][:].rearrange("p (t s) -> p s t", t=PLACES),
+            ks_listed[:].rearrange("p (s t) -> p s t", t=PLACES),
         )
+        nc.sync.dma_start(k_plane[1][0 : P - 4, :].bitcast(I32), k_plane[0][4:P, :].bitcast(I32))
+        v_window.extend(load_values(j) for j in range(1, PLACES))
 
-        kg = keep.tile([P, N], U32, name="kg")
-        nc.vector.tensor_copy(kg[:], kw[:].bitcast(U32).indirect(offsets[:]))
-        k16 = [keep.tile([P, 2 * N], U8, name=f"k16_{o}", align_bytes=64) for o in range(2)]
-        for o in range(2):
+        kw_listed = tile([P, N], U32, "kw_listed")
+        nc.vector.tensor_copy(kw_listed[:], kw_window[:].bitcast(U32).indirect(offsets[:]))
+
+        def key_words(o):
+            words = tile([P, 2 * N], U8, f"k_words{o}")
             nc.vector.tensor_copy(
-                k16[o][:].bitcast(U16).rearrange("p (t b i) -> p t b i", t=4, i=8),
-                kg[:].bitcast(U16).rearrange("p (b t i o) -> p o t b i", t=4, i=8, o=2)[:, o],
+                words[:].bitcast(U16).rearrange("p (t s) -> p s t", t=PLACES),
+                kw_listed[:].bitcast(U16).rearrange("p (s t o) -> p o s t", t=PLACES, o=2)[:, o],
             )
-        banks = [psum.tile([P, NQ], F32, name=f"bank{t}") for t in range(4)]
+            return words
 
-        def scores(o):
-            for t in range(4):
+        score = [psum.tile([P, NQ], F32, name=f"bank{t}") for t in range(PLACES)]
+
+        def score_pass(o, words, codes_name):
+            codes = tile([P, NQ], U32, codes_name)
+            scales = tile([P, NQ], U8, f"q_scales{o}")
+            quantize(nc, codes[:], scales[:], q_woven[o][:])
+            for t in range(PLACES):
                 nc.tensor.matmul_mx(
-                    out=banks[t][:],
-                    lhsT=k16[o][:, 256 * t : 256 * (t + 1)].bitcast(FP4X4),
-                    lhsT_scale=ksd[:, o, P * t : P * (t + 1)],
-                    rhs=q_codes[o][:].bitcast(FP8X4),
-                    rhs_scale=q_sc[o][:],
+                    out=score[t][:],
+                    lhsT=words[:, 2 * P * t : 2 * P * (t + 1)].bitcast(FP4X4),
+                    lhsT_scale=k_plane[o][:, P * t : P * (t + 1)],
+                    rhs=codes[:].bitcast(FP8X4),
+                    rhs_scale=scales[:],
                     start=(o == 0),
                     stop=(o == 1),
                 )
 
-        scores(0)
-        QS = 512
-        weave(nc.scalar.copy, q_bf[1][:, 0:QS, :], q1_raw[:, :, 0:QS])
-        quantize(nc, q_codes[1][:], q_sc[1][:], q_bf[1][:])
-        scores(1)
+        score_pass(0, key_words(0), "kw_window")
+        words1 = key_words(1)
+        weave(nc.scalar.copy, q_woven[1][:, 0:Q_SCALAR, :], q_raw[1][:, :, 0:Q_SCALAR])
+        weave(nc.vector.tensor_copy, q_woven[1][:, Q_SCALAR:NQ, :], q_raw[1][:, :, Q_SCALAR:NQ])
+        score_pass(1, words1, "q_codes1")
 
-        v_codes, v_sc = [], []
-
-        def values(j):
-            vg = keep.tile([P, 4, P], BF16, name=("vg0", "vg1", "sg1", "vg3")[j])
-            nc.vector.tensor_copy(vg[:].rearrange("p t (b i) -> p b t i", i=8), v_raw[j][:].indirect(offsets[:]))
-            vt_ps = psum.tile([P, 4, P], BF16, name=("bank3", "bank2", "vt_ps0", "vt_ps1")[j])
-            for t in range(4):
-                nc.tensor.transpose(vt_ps[:, t, :], vg[:, t, :], ident_b[:])
-            v_bf = keep.tile([P, P, 4], BF16, name=f"v_bf{j}", align_bytes=64)
-            nc.scalar.copy(v_bf[:], vt_ps[:].rearrange("p t m -> p m t"))
-            codes = keep.tile([P, P], U32, name=f"v_codes{j}", align_bytes=64)
-            sc = keep.tile([P, P], U8, name=f"v_sc{j}", align_bytes=64)
-            quantize(nc, codes[:], sc[:], v_bf[:])
-            v_codes.append(codes)
-            v_sc.append(sc)
-
-        y_codes = keep.tile([P, NQ], U32, name="y_codes", align_bytes=64)
-        y_sc = keep.tile([P, NQ], U8, name="y_sc", align_bytes=64)
+        sig = [tile([P, PLACES, HALF], F32, f"sig{h}") for h in range(2)]
         for h in range(2):
-            sg = keep.tile([P, 4, H], F32, name=f"sg{h}")
-            for t in range(4):
+            for t in range(PLACES):
                 nc.scalar.activation(
-                    sg[:, t, :], banks[t][:, H * h : H * (h + 1)], ACT.Sigmoid,
-                    bias=cols[:, 1, t : t + 1], scale=cols[:, 0, t : t + 1],
+                    sig[h][:, t, :],
+                    score[t][:, HALF * h : HALF * (h + 1)],
+                    SIGMOID,
+                    bias=kb_cols[:, t : t + 1],
+                    scale=ts_cols[:, t : t + 1],
                 )
-            y_bf = keep.tile([P, H, 4], BF16, name=f"y_bf{h}", align_bytes=64)
-            nc.vector.tensor_tensor(
-                y_bf[:].rearrange("p (c i) t -> p c t i", i=4),
-                sg[:].rearrange("p t (c i) -> p c t i", i=4),
-                cols[:, 2, 0:4].unsqueeze(1).unsqueeze(3).to_broadcast([P, H // 4, 4, 4]),
-                ALU.mult,
-            )
-            quantize(nc, y_codes[:, H * h : H * (h + 1)], y_sc[:, H * h : H * (h + 1)], y_bf[:])
-        for j in range(3):
-            values(j)
 
-        res = keep.tile([P, 4, NQ], F32, name="res")
-        out_rows = out_0.rearrange("(p j) q -> j p q", j=4)
-        for j in range(3):
-            acc = psum.tile([P, NQ], F32, name=("bank0", "bank1", "acc2")[j])
-            nc.tensor.matmul_mx(
-                out=acc[:], lhsT=v_codes[j][:].bitcast(FP8X4), lhsT_scale=v_sc[j][:],
-                rhs=y_codes[:].bitcast(FP8X4), rhs_scale=y_sc[:], start=True, stop=True,
-            )
-            nc.scalar.copy(res[:, j, :], acc[:])
-            nc.sync.dma_start(out_rows[j], res[:, j, :])
-        values(3)
-        o_codes = keep.tile([P, NQ], I32, name="o_codes", align_bytes=64)
-        o_sc = keep.tile([P, NQ], U8, name="o_sc", align_bytes=64)
-        o_bf = keep.tile([P, NQ, 4], BF16, name="o_bf", align_bytes=64)
-        words = out_1[0].rearrange("p q u -> p (q u)").bitcast(I32)
-        copies = (nc.vector.tensor_copy, nc.scalar.copy)
-        for h in range(2):
-            acc = psum.tile([P, H], F32, name=("bank3", "cols_ps")[h])
-            cs = slice(H * h, H * (h + 1))
-            nc.tensor.matmul_mx(
-                out=acc[:], lhsT=v_codes[3][:].bitcast(FP8X4), lhsT_scale=v_sc[3][:],
-                rhs=y_codes[:, cs].bitcast(FP8X4), rhs_scale=y_sc[:, cs], start=True, stop=True,
-            )
-            copies[h](res[:, 3, cs], acc[:])
-        nc.sync.dma_start(out_rows[3], res[:, 3, :])
-        TV = 64
-        weave(nc.vector.tensor_copy, o_bf[:, 0:H, :], res[:, :, 0:H])
-        weave(nc.scalar.copy, o_bf[:, H + TV : NQ, :], res[:, :, H + TV : NQ])
-        quantize(nc, o_codes[:, 0:H], o_sc[:, 0:H], o_bf[:, 0:H, :])
-        nc.sync.dma_start(words[:, 0:H], o_codes[:, 0:H])
-        weave(nc.vector.tensor_copy, o_bf[:, H : H + TV, :], res[:, :, H : H + TV])
-        quantize(nc, o_codes[:, H:NQ], o_sc[:, H:NQ], o_bf[:, H:NQ, :])
-        nc.sync.dma_start(words[:, H:NQ], o_codes[:, H:NQ])
+        def scale_on_vector(h, name):
+            scaled = tile([P, PLACES, HALF], BF16, name)
+            for t in range(PLACES):
+                nc.vector.tensor_scalar(scaled[:, t, :], sig[h][:, t, :], us_cols[:, t : t + 1], None, MULT)
+            return scaled
+
+        def scale_on_scalar(h, name):
+            scaled = tile([P, PLACES, HALF], BF16, name)
+            for t in range(PLACES):
+                nc.scalar.activation(scaled[:, t, :], sig[h][:, t, :], COPY, scale=us_cols[:, t : t + 1])
+            return scaled
+
+        def weave_weights(scaled, name):
+            woven = tile([P, HALF, PLACES], BF16, name)
+            weave(nc.vector.tensor_copy, woven[:], scaled[:])
+            return woven
+
+        def quantize_weights(h, woven, name):
+            codes = tile([P, HALF], U32, name)
+            scales = tile([P, HALF], U8, f"y_scales{h}")
+            quantize(nc, codes[:], scales[:], woven[:])
+            return codes, scales
+
+        def gather_values(j, name):
+            listed = tile([P, N], BF16, name)
+            nc.vector.tensor_copy(listed[:], v_window[j][:].indirect(offsets[:]))
+            return listed
+
+        v_woven = [tile([P, 2, P, PLACES], BF16, f"v_woven{pair}") for pair in range(2)]
+
+        def turn_values(j, listed):
+            words = listed[:].bitcast(F32)
+            turned = psum.tile([P, 2, P], F32, name=f"turn{j % 2}")
+            for u in range(2):
+                nc.tensor.transpose(turned[:, u, :], words[:, u : N // 2 : 2], identity[:])
+            nc.scalar.copy(v_woven[j // 2][:, j % 2].bitcast(F32), turned[:].rearrange("p u m -> p m u"))
+
+        def quantize_values(pair, name):
+            codes = tile([P, 2 * P], U32, name)
+            scales = tile([P, 2 * P], U8, f"v_scales{pair}")
+            quantize(nc, codes[:], scales[:], v_woven[pair][:].rearrange("p x m t -> p (x m) t"))
+            return codes, scales
+
+        listed0 = gather_values(0, "q_woven1")
+        listed1 = gather_values(1, "v_listed1")
+        y0_scaled = scale_on_vector(0, "v_window1")
+        y0 = quantize_weights(0, weave_weights(y0_scaled, "y_woven0"), "y_codes0")
+        listed2 = gather_values(2, "v_listed2")
+        turn_values(0, listed0)
+        turn_values(1, listed1)
+        y1_scaled = scale_on_scalar(1, "v_listed1")
+        v01 = quantize_values(0, "v_window2")
+        listed3 = gather_values(3, "v_listed3")
+        y1_woven = weave_weights(y1_scaled, "v_window3")
+        y1 = quantize_weights(1, y1_woven, "y_codes1")
+        turn_values(2, listed2)
+        turn_values(3, listed3)
+        v23 = quantize_values(1, "v_codes23")
+
+        out_rows = out_0.rearrange("(p j) q -> p j q", j=PLACES)
+        result = [tile([P, PLACES, HALF], F32, f"result{h}") for h in range(2)]
+        for h, (y_codes, y_scales) in enumerate((y0, y1)):
+            for pair, (v_codes, v_scales) in enumerate((v01, v23)):
+                acc = psum.tile([P, 2, HALF], F32, name=f"bank{2 * h + pair}")
+                for x in range(2):
+                    nc.tensor.matmul_mx(
+                        out=acc[:, x, :],
+                        lhsT=v_codes[:, P * x : P * (x + 1)].bitcast(FP8X4),
+                        lhsT_scale=v_scales[:, P * x : P * (x + 1)],
+                        rhs=y_codes[:].bitcast(FP8X4),
+                        rhs_scale=y_scales[:],
+                        start=True,
+                        stop=True,
+                    )
+                rows = slice(2 * pair, 2 * pair + 2)
+                nc.scalar.copy(result[h][:, rows, :], acc[:])
+                nc.sync.dma_start(out_rows[:, rows, HALF * h : HALF * (h + 1)], result[h][:, rows, :])
+
+        out_words = out_1[0].rearrange("p q u -> p (q u)").bitcast(I32)
+        o_codes = tile([P, NQ], I32, "o_codes")
+        o_scales = tile([P, NQ], U8, "o_scales")
+        o_woven = [tile([P, HALF, PLACES], BF16, f"o_woven{h}") for h in range(2)]
+
+        def hand_on(h):
+            cols = slice(HALF * h, HALF * (h + 1))
+            quantize(nc, o_codes[:, cols], o_scales[:, cols], o_woven[h][:])
+            nc.sync.dma_start(out_words[:, cols], o_codes[:, cols])
+
+        weave(nc.vector.tensor_copy, o_woven[0][:], result[0][:])
+        hand_on(0)
+        weave(nc.scalar.copy, o_woven[1][:, 0:OUT_SCALAR, :], result[1][:, :, 0:OUT_SCALAR])
+        weave(nc.vector.tensor_copy, o_woven[1][:, OUT_SCALAR:HALF, :], result[1][:, :, OUT_SCALAR:HALF])
+        hand_on(1)
         for Q in range(4):
             (nc.scalar, nc.sync)[Q % 2].dma_start(
-                out_2[0, 4 * Q : 4 * Q + 4, :].bitcast(I32), o_sc[32 * Q : 32 * Q + 4, :].bitcast(I32)
+                out_2[0, 4 * Q : 4 * Q + 4, :].bitcast(I32), o_scales[32 * Q : 32 * Q + 4, :].bitcast(I32)
             )

@@ -19,9 +19,9 @@ P = 128
 PLACES = 4
 N, T, D, NQ, DV = 512, 2048, 1024, 512, 512
 HALF = NQ // 2
+QUARTER = NQ // 4
 LAST = P - 1
-Q_SCALAR = 320
-OUT_SCALAR = 128
+SHIFT = 16
 
 FLOPS = 2 * N * NQ * (D + DV)
 BYTES = 4 * D * NQ + 4 * P * T + 32 * T + 4 * DV * T + 8 * T + 4 * N + 2 * P * (N // 16) + 5 * DV * NQ + 16 * NQ
@@ -48,53 +48,60 @@ def tile_attend_plo_sigb_topk_kernel(tc, qT, k_words, k_scales, vT, ts, kb, us, 
         nc.sync.dma_start(offsets[:], offs)
         ks_window = tile([P, T], U8, "ks_window")
         nc.gpsimd.memset(ks_window[:].bitcast(I32), 0)
-        warm = tile([P, 2], F32, "warm")
-        nc.gpsimd.memset(warm[:, 0:1], 0.0)
         ts_window = tile([P, T], F32, "ts_window")
         nc.scalar.dma_start(ts_window[LAST:P, :], ts[0:1, :])
-        nc.vector.memset(ts_window[0:LAST, :].bitcast(I32), 0)
+        for cols in (slice(0, T // 2 - 1), slice(T // 2 - 1, T)):
+            nc.vector.memset(ts_window[0:LAST, cols].bitcast(I32), 0)
         kb_window = tile([P, T], F32, "kb_window")
+        nc.sync.dma_start(kb_window[LAST:P, :], kb[0:1, :])
         nc.gpsimd.memset(kb_window[0:LAST, :].bitcast(I32), 0)
-        nc.scalar.dma_start(kb_window[LAST:P, :], kb[0:1, :])
-        q_rows = qT[0].rearrange("(o p t) w -> o p t w", o=2, t=PLACES)
-        q_raw = [tile([P, PLACES, NQ], F32, f"q_raw{o}") for o in range(2)]
-        nc.sync.dma_start(q_raw[0][:], q_rows[0])
-        for Q in range(4):
-            nc.sync.dma_start(
-                ks_window[32 * Q : 32 * Q + 8, :].bitcast(I32), k_scales[:, 4 * Q : 4 * Q + 4, :].bitcast(I32)
-            )
-        kw_window = tile([P, T], I32, "kw_window")
-        nc.sync.dma_start(kw_window[:], k_words[0].rearrange("p t b -> p (t b)").bitcast(I32))
-        us_cols = tile([P, PLACES], F32, "us_cols")
-        nc.sync.dma_start(us_cols[:], us[0].rearrange("(p t) z -> p (t z)", t=PLACES))
-        nc.sync.dma_start(q_raw[1][:], q_rows[1])
-        v_rows = vT.rearrange("(p j) t -> j p t", j=PLACES)
-
-        def load_values(j):
-            window = tile([P, T], F32, f"v_window{j}")
-            nc.sync.dma_start(window[:], v_rows[j])
-            return window
-
-        v_window = [load_values(0)]
+        warm = tile([P, 2], F32, "warm")
+        nc.gpsimd.memset(warm[:, 0:1], 0.0)
         nc.scalar.activation(warm[:, 1:2], warm[:, 0:1], SIGMOID)
         identity = tile([P, P], F32, "identity")
         make_identity(nc, identity[:])
 
-        q_woven = [tile([P, NQ, PLACES], BF16, f"q_woven{o}") for o in range(2)]
-        weave(nc.scalar.copy, q_woven[0][:], q_raw[0][:])
+        q_rows = qT[0].rearrange("(o p t) w -> o p t w", o=2, t=PLACES)
+        kw_window = tile([P, T], I32, "kw_window")
+        nc.sync.dma_start(kw_window[:], k_words[0].rearrange("p t b -> p (t b)").bitcast(I32))
+        ks_rows = k_scales.rearrange("o (Q r) t -> r Q o t", r=4)
+        for r in range(4):
+            nc.sync.dma_start(ks_window[r:P:SHIFT, :].bitcast(I32), ks_rows[r].bitcast(I32))
+        q_raw = [[tile([P, PLACES, HALF], F32, f"q_raw{o}{h}") for h in range(2)] for o in range(2)]
+        for o in range(2):
+            for h in range(2):
+                nc.sync.dma_start(q_raw[o][h][:], q_rows[o][:, :, HALF * h : HALF * (h + 1)])
 
-        def token_columns(window, name, bank):
-            listed = tile([P, N], F32, name + "_listed")
+        q_woven = [tile([P, NQ, PLACES], BF16, f"q_woven{o}") for o in range(2)]
+        q_codes = [tile([P, NQ], U32, name) for name in ("kw_window", "q_codes1")]
+        q_scales = [tile([P, NQ], U8, f"q_scales{o}") for o in range(2)]
+
+        def weave_queries(o, h):
+            weave(nc.scalar.copy, q_woven[o][:, HALF * h : HALF * (h + 1), :], q_raw[o][h][:])
+
+        def quantize_queries(o, h):
+            cols = slice(HALF * h, HALF * (h + 1))
+            quantize(nc, q_codes[o][:, cols], q_scales[o][:, cols], q_woven[o][:, cols, :])
+
+        def token_columns(window, listed_name, bank):
+            listed = tile([P, N], F32, listed_name)
             nc.vector.tensor_copy(listed[:], window[:].indirect(offsets[:]))
             turned = psum.tile([P, PLACES, P], F32, name=bank)
             for t in range(PLACES):
                 nc.tensor.transpose(turned[:, t, :], listed[:, t:N:PLACES], identity[:])
-            columns = tile([P, PLACES], F32, name + "_cols")
+            return turned
+
+        def copy_columns(turned, name):
+            columns = tile([P, PLACES], F32, name)
             nc.scalar.copy(columns[:], turned[:, :, LAST])
             return columns
 
-        ts_cols = token_columns(ts_window, "ts", "turn0")
-        kb_cols = token_columns(kb_window, "kb", "turn1")
+        ts_turned = token_columns(ts_window, "ts_listed", "turn0")
+        ts_cols = copy_columns(ts_turned, "ts_cols")
+        kb_turned = token_columns(kb_window, "kb_listed", "turn1")
+        weave_queries(0, 0)
+        kb_cols = copy_columns(kb_turned, "q_raw00")
+        weave_queries(0, 1)
 
         ks_listed = tile([P, N], U8, "ks_listed")
         nc.vector.tensor_copy(ks_listed[:], ks_window[:].indirect(offsets[:]))
@@ -103,10 +110,15 @@ def tile_attend_plo_sigb_topk_kernel(tc, qT, k_words, k_scales, vT, ts, kb, us, 
             k_plane[0][:].rearrange("p (t s) -> p s t", t=PLACES),
             ks_listed[:].rearrange("p (s t) -> p s t", t=PLACES),
         )
-        nc.sync.dma_start(k_plane[1][0 : P - 4, :].bitcast(I32), k_plane[0][4:P, :].bitcast(I32))
-        v_window.extend(load_values(j) for j in range(1, PLACES))
+        nc.sync.dma_start(k_plane[1][0 : P - SHIFT, :].bitcast(I32), k_plane[0][SHIFT:P, :].bitcast(I32))
+        us_cols = tile([P, PLACES], F32, "us_cols")
+        nc.sync.dma_start(us_cols[:], us[0].rearrange("(p t) z -> p (t z)", t=PLACES))
+        v_rows = vT.rearrange("(p j) t -> j p t", j=PLACES)
+        v_window = [tile([P, T], F32, f"v_window{j}") for j in range(PLACES)]
+        for j in range(PLACES):
+            nc.sync.dma_start(v_window[j][:], v_rows[j])
 
-        kw_listed = tile([P, N], U32, "kw_listed")
+        kw_listed = tile([P, N], U32, "ks_window")
         nc.vector.tensor_copy(kw_listed[:], kw_window[:].bitcast(U32).indirect(offsets[:]))
 
         def key_words(o):
@@ -117,133 +129,115 @@ def tile_attend_plo_sigb_topk_kernel(tc, qT, k_words, k_scales, vT, ts, kb, us, 
             )
             return words
 
-        score = [psum.tile([P, NQ], F32, name=f"bank{t}") for t in range(PLACES)]
+        words = [key_words(o) for o in range(2)]
+        for h in range(2):
+            quantize_queries(0, h)
+        for h in range(2):
+            weave_queries(1, h)
+            quantize_queries(1, h)
 
-        def score_pass(o, words, codes_name):
-            codes = tile([P, NQ], U32, codes_name)
-            scales = tile([P, NQ], U8, f"q_scales{o}")
-            quantize(nc, codes[:], scales[:], q_woven[o][:])
+        score = [psum.tile([P, NQ], F32, name=f"bank{t}") for t in range(PLACES)]
+        for o in range(2):
             for t in range(PLACES):
                 nc.tensor.matmul_mx(
                     out=score[t][:],
-                    lhsT=words[:, 2 * P * t : 2 * P * (t + 1)].bitcast(FP4X4),
+                    lhsT=words[o][:, 2 * P * t : 2 * P * (t + 1)].bitcast(FP4X4),
                     lhsT_scale=k_plane[o][:, P * t : P * (t + 1)],
-                    rhs=codes[:].bitcast(FP8X4),
-                    rhs_scale=scales[:],
+                    rhs=q_codes[o][:].bitcast(FP8X4),
+                    rhs_scale=q_scales[o][:],
                     start=(o == 0),
                     stop=(o == 1),
                 )
+        sig = [tile([P, NQ], F32, f"sig{t}") for t in range(PLACES)]
+        for t in range(PLACES):
+            nc.scalar.activation(
+                sig[t][:], score[t][:], SIGMOID, bias=kb_cols[:, t : t + 1], scale=ts_cols[:, t : t + 1]
+            )
 
-        score_pass(0, key_words(0), "kw_window")
-        words1 = key_words(1)
-        weave(nc.scalar.copy, q_woven[1][:, 0:Q_SCALAR, :], q_raw[1][:, :, 0:Q_SCALAR])
-        weave(nc.vector.tensor_copy, q_woven[1][:, Q_SCALAR:NQ, :], q_raw[1][:, :, Q_SCALAR:NQ])
-        score_pass(1, words1, "q_codes1")
-
-        sig = [tile([P, PLACES, HALF], F32, f"sig{h}") for h in range(2)]
-        for h in range(2):
-            for t in range(PLACES):
-                nc.scalar.activation(
-                    sig[h][:, t, :],
-                    score[t][:, HALF * h : HALF * (h + 1)],
-                    SIGMOID,
-                    bias=kb_cols[:, t : t + 1],
-                    scale=ts_cols[:, t : t + 1],
-                )
-
-        def scale_on_vector(h, name):
-            scaled = tile([P, PLACES, HALF], BF16, name)
-            for t in range(PLACES):
-                nc.vector.tensor_scalar(scaled[:, t, :], sig[h][:, t, :], us_cols[:, t : t + 1], None, MULT)
-            return scaled
-
-        def scale_on_scalar(h, name):
-            scaled = tile([P, PLACES, HALF], BF16, name)
-            for t in range(PLACES):
-                nc.scalar.activation(scaled[:, t, :], sig[h][:, t, :], COPY, scale=us_cols[:, t : t + 1])
-            return scaled
-
-        def weave_weights(scaled, name):
-            woven = tile([P, HALF, PLACES], BF16, name)
-            weave(nc.vector.tensor_copy, woven[:], scaled[:])
-            return woven
-
-        def quantize_weights(h, woven, name):
-            codes = tile([P, HALF], U32, name)
-            scales = tile([P, HALF], U8, f"y_scales{h}")
-            quantize(nc, codes[:], scales[:], woven[:])
-            return codes, scales
-
-        def gather_values(j, name):
-            listed = tile([P, N], BF16, name)
+        def gather_values(j):
+            listed = tile([P, N], BF16, f"v_listed{j}")
             nc.vector.tensor_copy(listed[:], v_window[j][:].indirect(offsets[:]))
             return listed
 
-        v_woven = [tile([P, 2, P, PLACES], BF16, f"v_woven{pair}") for pair in range(2)]
-
-        def turn_values(j, listed):
-            words = listed[:].bitcast(F32)
-            turned = psum.tile([P, 2, P], F32, name=f"turn{j % 2}")
+        def turn_values(j, listed, woven):
+            pairs = listed[:].bitcast(F32)
+            turned = psum.tile([P, 2, P], F32, name=f"turn{j}")
             for u in range(2):
-                nc.tensor.transpose(turned[:, u, :], words[:, u : N // 2 : 2], identity[:])
-            nc.scalar.copy(v_woven[j // 2][:, j % 2].bitcast(F32), turned[:].rearrange("p u m -> p m u"))
+                nc.tensor.transpose(turned[:, u, :], pairs[:, u : N // 2 : 2], identity[:])
+            nc.scalar.copy(woven.bitcast(F32), turned[:].rearrange("p u m -> p m u"))
 
-        def quantize_values(pair, name):
-            codes = tile([P, 2 * P], U32, name)
-            scales = tile([P, 2 * P], U8, f"v_scales{pair}")
-            quantize(nc, codes[:], scales[:], v_woven[pair][:].rearrange("p x m t -> p (x m) t"))
-            return codes, scales
+        v_woven01 = tile([P, 2 * P, PLACES], BF16, "v_woven01")
+        v_woven23 = [tile([P, P, PLACES], BF16, f"v_woven{j}") for j in (2, 3)]
 
-        listed0 = gather_values(0, "q_woven1")
-        listed1 = gather_values(1, "v_listed1")
-        y0_scaled = scale_on_vector(0, "v_window1")
-        y0 = quantize_weights(0, weave_weights(y0_scaled, "y_woven0"), "y_codes0")
-        listed2 = gather_values(2, "v_listed2")
-        turn_values(0, listed0)
-        turn_values(1, listed1)
-        y1_scaled = scale_on_scalar(1, "v_listed1")
-        v01 = quantize_values(0, "v_window2")
-        listed3 = gather_values(3, "v_listed3")
-        y1_woven = weave_weights(y1_scaled, "v_window3")
-        y1 = quantize_weights(1, y1_woven, "y_codes1")
-        turn_values(2, listed2)
-        turn_values(3, listed3)
-        v23 = quantize_values(1, "v_codes23")
+        listed0 = gather_values(0)
+        scaled = tile([P, PLACES, NQ], BF16, "v_window0")
+        for t in range(PLACES - 1):
+            nc.vector.tensor_scalar(scaled[:, t, :], sig[t][:], us_cols[:, t : t + 1], None, MULT)
+        turn_values(0, listed0, v_woven01[:, 0:P, :])
+        nc.scalar.activation(scaled[:, 3, :], sig[3][:], COPY, scale=us_cols[:, 3:4])
+        listed1 = gather_values(1)
+        turn_values(1, listed1, v_woven01[:, P : 2 * P, :])
+        y_woven = [tile([P, HALF, PLACES], BF16, name) for name in ("v_window1", "y_woven1")]
+        weave(nc.vector.tensor_copy, y_woven[0][:], scaled[:, :, 0:HALF])
+        weave(nc.scalar.copy, y_woven[1][:], scaled[:, :, HALF:NQ])
+        listed2 = gather_values(2)
+        turn_values(2, listed2, v_woven23[0][:])
+        codes = tile([P, NQ + 2 * P], U32, "v_window2")
+        y_codes = codes[:, 0:NQ]
+        y_scales = tile([P, NQ], U8, "y_scales")
+        v_scales = tile([P, DV], U8, "v_scales")
+        quantize(nc, y_codes[:, 0:HALF], y_scales[:, 0:HALF], y_woven[0][:])
+        quantize(nc, codes[:, NQ : NQ + 2 * P], v_scales[:, 0 : 2 * P], v_woven01[:])
+        quantize(nc, y_codes[:, HALF:NQ], y_scales[:, HALF:NQ], y_woven[1][:])
+        listed3 = gather_values(3)
+        turn_values(3, listed3, v_woven23[1][:])
+        v2_codes = tile([P, P], U32, "v_window3")
+        v3_codes = tile([P, P], U32, "v3_codes")
+        quantize(nc, v2_codes[:], v_scales[:, 2 * P : 3 * P], v_woven23[0][:])
+        quantize(nc, v3_codes[:], v_scales[:, 3 * P : 4 * P], v_woven23[1][:])
+        v_codes = [codes[:, NQ : NQ + P], codes[:, NQ + P : NQ + 2 * P], v2_codes[:], v3_codes[:]]
 
         out_rows = out_0.rearrange("(p j) q -> p j q", j=PLACES)
-        result = [tile([P, PLACES, HALF], F32, f"result{h}") for h in range(2)]
-        for h, (y_codes, y_scales) in enumerate((y0, y1)):
-            for pair, (v_codes, v_scales) in enumerate((v01, v23)):
-                acc = psum.tile([P, 2, HALF], F32, name=f"bank{2 * h + pair}")
-                for x in range(2):
+        acc = [psum.tile([P, PLACES, QUARTER], F32, name=f"bank{c}") for c in range(4)]
+
+        def products(js):
+            for c in range(4):
+                cols = slice(QUARTER * c, QUARTER * (c + 1))
+                for j in js:
                     nc.tensor.matmul_mx(
-                        out=acc[:, x, :],
-                        lhsT=v_codes[:, P * x : P * (x + 1)].bitcast(FP8X4),
-                        lhsT_scale=v_scales[:, P * x : P * (x + 1)],
-                        rhs=y_codes[:].bitcast(FP8X4),
-                        rhs_scale=y_scales[:],
+                        out=acc[c][:, j, :],
+                        lhsT=v_codes[j].bitcast(FP8X4),
+                        lhsT_scale=v_scales[:, P * j : P * (j + 1)],
+                        rhs=y_codes[:, cols].bitcast(FP8X4),
+                        rhs_scale=y_scales[:, cols],
                         start=True,
                         stop=True,
                     )
-                rows = slice(2 * pair, 2 * pair + 2)
-                nc.scalar.copy(result[h][:, rows, :], acc[:])
-                nc.sync.dma_start(out_rows[:, rows, HALF * h : HALF * (h + 1)], result[h][:, rows, :])
+
+        def store_rows(j0, j1):
+            result = tile([P, j1 - j0, NQ], F32, f"result{j0}")
+            for c in range(4):
+                nc.scalar.copy(result[:, :, QUARTER * c : QUARTER * (c + 1)], acc[c][:, j0:j1, :])
+            nc.sync.dma_start(out_rows[:, j0:j1, :], result[:])
+
+        products((0, 1))
+        store_rows(0, 2)
+        products((2,))
+        store_rows(2, 3)
+        products((3,))
 
         out_words = out_1[0].rearrange("p q u -> p (q u)").bitcast(I32)
         o_codes = tile([P, NQ], I32, "o_codes")
         o_scales = tile([P, NQ], U8, "o_scales")
         o_woven = [tile([P, HALF, PLACES], BF16, f"o_woven{h}") for h in range(2)]
-
-        def hand_on(h):
+        for c in range(4):
+            copy = (nc.vector.tensor_copy, nc.scalar.copy)[c % 2]
+            copy(o_woven[c // 2][:, QUARTER * (c % 2) : QUARTER * (c % 2 + 1), :], acc[c][:].rearrange("p j n -> p n j"))
+        for h in range(2):
             cols = slice(HALF * h, HALF * (h + 1))
             quantize(nc, o_codes[:, cols], o_scales[:, cols], o_woven[h][:])
             nc.sync.dma_start(out_words[:, cols], o_codes[:, cols])
-
-        weave(nc.vector.tensor_copy, o_woven[0][:], result[0][:])
-        hand_on(0)
-        weave(nc.scalar.copy, o_woven[1][:, 0:OUT_SCALAR, :], result[1][:, :, 0:OUT_SCALAR])
-        weave(nc.vector.tensor_copy, o_woven[1][:, OUT_SCALAR:HALF, :], result[1][:, :, OUT_SCALAR:HALF])
-        hand_on(1)
+        store_rows(3, 4)
         for Q in range(4):
             (nc.scalar, nc.sync)[Q % 2].dma_start(
                 out_2[0, 4 * Q : 4 * Q + 4, :].bitcast(I32), o_scales[32 * Q : 32 * Q + 4, :].bitcast(I32)

@@ -68,16 +68,16 @@ def tile_attend_plo_sigb_topk_kernel(tc, qT, k_words, k_scales, vT, ts, kb, us, 
         for r in range(4):
             nc.sync.dma_start(ks_window[r:P:SHIFT, :].bitcast(I32), ks_rows[r].bitcast(I32))
         q_raw = [[tile([P, PLACES, HALF], F32, f"q_raw{o}{h}") for h in range(2)] for o in range(2)]
-        for o in range(2):
-            for h in range(2):
+        for h in range(2):
+            for o in range(2):
                 nc.sync.dma_start(q_raw[o][h][:], q_rows[o][:, :, HALF * h : HALF * (h + 1)])
 
         q_woven = [tile([P, NQ, PLACES], BF16, f"q_woven{o}") for o in range(2)]
         q_codes = [tile([P, NQ], U32, name) for name in ("kw_window", "q_codes1")]
         q_scales = [tile([P, NQ], U8, f"q_scales{o}") for o in range(2)]
 
-        def weave_queries(o, h):
-            weave(nc.scalar.copy, q_woven[o][:, HALF * h : HALF * (h + 1), :], q_raw[o][h][:])
+        def weave_queries(o, h, copy):
+            weave(copy, q_woven[o][:, HALF * h : HALF * (h + 1), :], q_raw[o][h][:])
 
         def quantize_queries(o, h):
             cols = slice(HALF * h, HALF * (h + 1))
@@ -96,12 +96,13 @@ def tile_attend_plo_sigb_topk_kernel(tc, qT, k_words, k_scales, vT, ts, kb, us, 
             nc.scalar.copy(columns[:], turned[:, :, LAST])
             return columns
 
-        ts_turned = token_columns(ts_window, "ts_listed", "turn0")
+        ts_turned = token_columns(ts_window, "ts_listed", "bank10")
         ts_cols = copy_columns(ts_turned, "ts_cols")
-        kb_turned = token_columns(kb_window, "kb_listed", "turn1")
-        weave_queries(0, 0)
+        kb_turned = token_columns(kb_window, "kb_listed", "bank11")
+        weave_queries(0, 0, nc.scalar.copy)
         kb_cols = copy_columns(kb_turned, "q_raw00")
-        weave_queries(0, 1)
+        weave_queries(1, 0, nc.scalar.copy)
+        weave_queries(0, 1, nc.scalar.copy)
 
         ks_listed = tile([P, N], U8, "ks_listed")
         nc.vector.tensor_copy(ks_listed[:], ks_window[:].indirect(offsets[:]))
@@ -130,29 +131,37 @@ def tile_attend_plo_sigb_topk_kernel(tc, qT, k_words, k_scales, vT, ts, kb, us, 
             return words
 
         words = [key_words(o) for o in range(2)]
-        for h in range(2):
-            quantize_queries(0, h)
-        for h in range(2):
-            weave_queries(1, h)
-            quantize_queries(1, h)
 
-        score = [psum.tile([P, NQ], F32, name=f"bank{t}") for t in range(PLACES)]
-        for o in range(2):
+        def sigmoids(h):
+            sig = []
             for t in range(PLACES):
-                nc.tensor.matmul_mx(
-                    out=score[t][:],
-                    lhsT=words[o][:, 2 * P * t : 2 * P * (t + 1)].bitcast(FP4X4),
-                    lhsT_scale=k_plane[o][:, P * t : P * (t + 1)],
-                    rhs=q_codes[o][:].bitcast(FP8X4),
-                    rhs_scale=q_scales[o][:],
-                    start=(o == 0),
-                    stop=(o == 1),
-                )
-        sig = [tile([P, NQ], F32, f"sig{t}") for t in range(PLACES)]
-        for t in range(PLACES):
-            nc.scalar.activation(
-                sig[t][:], score[t][:], SIGMOID, bias=kb_cols[:, t : t + 1], scale=ts_cols[:, t : t + 1]
-            )
+                score = psum.tile([P, HALF], F32, name=f"bank{h}{t}")
+                for x in range(2):
+                    cols = slice(HALF * h + QUARTER * x, HALF * h + QUARTER * (x + 1))
+                    for o in range(2):
+                        nc.tensor.matmul_mx(
+                            out=score[:, QUARTER * x : QUARTER * (x + 1)],
+                            lhsT=words[o][:, 2 * P * t : 2 * P * (t + 1)].bitcast(FP4X4),
+                            lhsT_scale=k_plane[o][:, P * t : P * (t + 1)],
+                            rhs=q_codes[o][:, cols].bitcast(FP8X4),
+                            rhs_scale=q_scales[o][:, cols],
+                            start=(o == 0),
+                            stop=(o == 1),
+                        )
+                out = tile([P, HALF], F32, f"sig{h}{t}")
+                nc.scalar.activation(out[:], score[:], SIGMOID, bias=kb_cols[:, t : t + 1], scale=ts_cols[:, t : t + 1])
+                sig.append(out)
+            return sig
+
+        quantize_queries(0, 0)
+        quantize_queries(1, 0)
+        sig0 = sigmoids(0)
+        scaled = [tile([P, PLACES, HALF], BF16, f"scaled{h}") for h in range(2)]
+        nc.scalar.activation(scaled[0][:, 3, :], sig0[3][:], COPY, scale=us_cols[:, 3:4])
+        quantize_queries(0, 1)
+        weave_queries(1, 1, nc.vector.tensor_copy)
+        quantize_queries(1, 1)
+        sig1 = sigmoids(1)
 
         def gather_values(j):
             listed = tile([P, N], BF16, f"v_listed{j}")
@@ -161,7 +170,7 @@ def tile_attend_plo_sigb_topk_kernel(tc, qT, k_words, k_scales, vT, ts, kb, us, 
 
         def turn_values(j, listed, woven):
             pairs = listed[:].bitcast(F32)
-            turned = psum.tile([P, 2, P], F32, name=f"turn{j}")
+            turned = psum.tile([P, 2, P], F32, name=f"bank0{j}")
             for u in range(2):
                 nc.tensor.transpose(turned[:, u, :], pairs[:, u : N // 2 : 2], identity[:])
             nc.scalar.copy(woven.bitcast(F32), turned[:].rearrange("p u m -> p m u"))
@@ -169,75 +178,79 @@ def tile_attend_plo_sigb_topk_kernel(tc, qT, k_words, k_scales, vT, ts, kb, us, 
         v_woven01 = tile([P, 2 * P, PLACES], BF16, "v_woven01")
         v_woven23 = [tile([P, P, PLACES], BF16, f"v_woven{j}") for j in (2, 3)]
 
-        listed0 = gather_values(0)
-        scaled = tile([P, PLACES, NQ], BF16, "v_window0")
         for t in range(PLACES - 1):
-            nc.vector.tensor_scalar(scaled[:, t, :], sig[t][:], us_cols[:, t : t + 1], None, MULT)
+            nc.vector.tensor_scalar(scaled[0][:, t, :], sig0[t][:], us_cols[:, t : t + 1], None, MULT)
+        listed0 = gather_values(0)
+        y_woven = [tile([P, HALF, PLACES], BF16, "v_window0")]
+        weave(nc.vector.tensor_copy, y_woven[0][:], scaled[0][:])
+        y_scales = tile([P, NQ], U8, "y_scales")
         turn_values(0, listed0, v_woven01[:, 0:P, :])
-        nc.scalar.activation(scaled[:, 3, :], sig[3][:], COPY, scale=us_cols[:, 3:4])
+        for t in range(PLACES):
+            nc.scalar.activation(scaled[1][:, t, :], sig1[t][:], COPY, scale=us_cols[:, t : t + 1])
         listed1 = gather_values(1)
+        y0_codes = tile([P, HALF], U32, "v_window1")
+        quantize(nc, y0_codes[:], y_scales[:, 0:HALF], y_woven[0][:])
         turn_values(1, listed1, v_woven01[:, P : 2 * P, :])
-        y_woven = [tile([P, HALF, PLACES], BF16, name) for name in ("v_window1", "y_woven1")]
-        weave(nc.vector.tensor_copy, y_woven[0][:], scaled[:, :, 0:HALF])
-        weave(nc.scalar.copy, y_woven[1][:], scaled[:, :, HALF:NQ])
+        y_woven.append(tile([P, HALF, PLACES], BF16, "v_listed1"))
+        weave(nc.scalar.copy, y_woven[1][:], scaled[1][:])
+        v_scales = tile([P, DV], U8, "v_scales")
         listed2 = gather_values(2)
         turn_values(2, listed2, v_woven23[0][:])
-        codes = tile([P, NQ + 2 * P], U32, "v_window2")
-        y_codes = codes[:, 0:NQ]
-        y_scales = tile([P, NQ], U8, "y_scales")
-        v_scales = tile([P, DV], U8, "v_scales")
-        quantize(nc, y_codes[:, 0:HALF], y_scales[:, 0:HALF], y_woven[0][:])
-        quantize(nc, codes[:, NQ : NQ + 2 * P], v_scales[:, 0 : 2 * P], v_woven01[:])
-        quantize(nc, y_codes[:, HALF:NQ], y_scales[:, HALF:NQ], y_woven[1][:])
+        codes = tile([P, HALF + 2 * P], U32, "v_window2")
+        v01_codes = codes[:, HALF : HALF + 2 * P]
+        quantize(nc, v01_codes, v_scales[:, 0 : 2 * P], v_woven01[:])
+        quantize(nc, codes[:, 0:HALF], y_scales[:, HALF:NQ], y_woven[1][:])
+        y_codes = [y0_codes[:], codes[:, 0:HALF]]
         listed3 = gather_values(3)
         turn_values(3, listed3, v_woven23[1][:])
         v2_codes = tile([P, P], U32, "v_window3")
         v3_codes = tile([P, P], U32, "v3_codes")
         quantize(nc, v2_codes[:], v_scales[:, 2 * P : 3 * P], v_woven23[0][:])
         quantize(nc, v3_codes[:], v_scales[:, 3 * P : 4 * P], v_woven23[1][:])
-        v_codes = [codes[:, NQ : NQ + P], codes[:, NQ + P : NQ + 2 * P], v2_codes[:], v3_codes[:]]
+        v_codes = [v01_codes[:, 0:P], v01_codes[:, P : 2 * P], v2_codes[:], v3_codes[:]]
 
         out_rows = out_0.rearrange("(p j) q -> p j q", j=PLACES)
-        acc = [psum.tile([P, PLACES, QUARTER], F32, name=f"bank{c}") for c in range(4)]
+        result = [tile([P, PLACES, HALF], F32, f"result{h}") for h in range(2)]
 
-        def products(js):
-            for c in range(4):
-                cols = slice(QUARTER * c, QUARTER * (c + 1))
-                for j in js:
-                    nc.tensor.matmul_mx(
-                        out=acc[c][:, j, :],
-                        lhsT=v_codes[j].bitcast(FP8X4),
-                        lhsT_scale=v_scales[:, P * j : P * (j + 1)],
-                        rhs=y_codes[:, cols].bitcast(FP8X4),
-                        rhs_scale=y_scales[:, cols],
-                        start=True,
-                        stop=True,
-                    )
+        def products(j0, j1, h, cols, bank):
+            acc = psum.tile([P, j1 - j0, cols.stop - cols.start], F32, name=bank)
+            for j in range(j0, j1):
+                nc.tensor.matmul_mx(
+                    out=acc[:, j - j0, :],
+                    lhsT=v_codes[j].bitcast(FP8X4),
+                    lhsT_scale=v_scales[:, P * j : P * (j + 1)],
+                    rhs=y_codes[h][:, cols].bitcast(FP8X4),
+                    rhs_scale=y_scales[:, HALF * h + cols.start : HALF * h + cols.stop],
+                    start=True,
+                    stop=True,
+                )
+            nc.scalar.copy(result[h][:, j0:j1, cols], acc[:])
 
-        def store_rows(j0, j1):
-            result = tile([P, j1 - j0, NQ], F32, f"result{j0}")
-            for c in range(4):
-                nc.scalar.copy(result[:, :, QUARTER * c : QUARTER * (c + 1)], acc[c][:, j0:j1, :])
-            nc.sync.dma_start(out_rows[:, j0:j1, :], result[:])
+        def store_rows(j0, j1, h):
+            nc.sync.dma_start(out_rows[:, j0:j1, HALF * h : HALF * (h + 1)], result[h][:, j0:j1, :])
 
-        products((0, 1))
-        store_rows(0, 2)
-        products((2,))
-        store_rows(2, 3)
-        products((3,))
+        for j0, j1 in ((0, 2), (2, 3)):
+            for h in range(2):
+                products(j0, j1, h, slice(0, HALF), f"bank1{j0 + h}")
+                store_rows(j0, j1, h)
+        quarters = [slice(QUARTER * x, QUARTER * (x + 1)) for x in range(2)]
+        for h in range(2):
+            for x in range(2):
+                products(3, 4, h, quarters[x], f"bank0{2 * h + x}")
+            store_rows(3, 4, h)
 
         out_words = out_1[0].rearrange("p q u -> p (q u)").bitcast(I32)
         o_codes = tile([P, NQ], I32, "o_codes")
         o_scales = tile([P, NQ], U8, "o_scales")
         o_woven = [tile([P, HALF, PLACES], BF16, f"o_woven{h}") for h in range(2)]
-        for c in range(4):
-            copy = (nc.vector.tensor_copy, nc.scalar.copy)[c % 2]
-            copy(o_woven[c // 2][:, QUARTER * (c % 2) : QUARTER * (c % 2 + 1), :], acc[c][:].rearrange("p j n -> p n j"))
+        for h in range(2):
+            for x in range(2):
+                copy = nc.scalar.copy if h + x == 2 else nc.vector.tensor_copy
+                weave(copy, o_woven[h][:, quarters[x], :], result[h][:, :, quarters[x]])
         for h in range(2):
             cols = slice(HALF * h, HALF * (h + 1))
             quantize(nc, o_codes[:, cols], o_scales[:, cols], o_woven[h][:])
             nc.sync.dma_start(out_words[:, cols], o_codes[:, cols])
-        store_rows(3, 4)
         for Q in range(4):
             (nc.scalar, nc.sync)[Q % 2].dma_start(
                 out_2[0, 4 * Q : 4 * Q + 4, :].bitcast(I32), o_scales[32 * Q : 32 * Q + 4, :].bitcast(I32)

@@ -21,7 +21,7 @@ N, T, D, NQ, DV = 512, 2048, 1024, 512, 512
 HALF = NQ // 2
 QUARTER = NQ // 4
 LAST = P - 1
-SHIFT = 16
+KS_ROW = P - 32
 
 FLOPS = 2 * N * NQ * (D + DV)
 BYTES = 4 * D * NQ + 4 * P * T + 32 * T + 4 * DV * T + 8 * T + 4 * N + 2 * P * (N // 16) + 5 * DV * NQ + 16 * NQ
@@ -47,7 +47,8 @@ def tile_attend_plo_sigb_topk_kernel(tc, qT, k_words, k_scales, vT, ts, kb, us, 
         offsets = tile([P, N // 16], U16, "offsets")
         nc.sync.dma_start(offsets[:], offs)
         ks_window = tile([P, T], U8, "ks_window")
-        nc.gpsimd.memset(ks_window[:].bitcast(I32), 0)
+        nc.sync.dma_start(ks_window[KS_ROW:P, :].bitcast(I32), k_scales.rearrange("o f t -> f o t").bitcast(I32))
+        nc.gpsimd.memset(ks_window[0:KS_ROW, :].bitcast(I32), 0)
         ts_window = tile([P, T], F32, "ts_window")
         nc.scalar.dma_start(ts_window[LAST:P, :], ts[0:1, :])
         for cols in (slice(0, T // 2 - 1), slice(T // 2 - 1, T)):
@@ -64,16 +65,17 @@ def tile_attend_plo_sigb_topk_kernel(tc, qT, k_words, k_scales, vT, ts, kb, us, 
         q_rows = qT[0].rearrange("(o p t) w -> o p t w", o=2, t=PLACES)
         kw_window = tile([P, T], I32, "kw_window")
         nc.sync.dma_start(kw_window[:], k_words[0].rearrange("p t b -> p (t b)").bitcast(I32))
-        ks_rows = k_scales.rearrange("o (Q r) t -> r Q o t", r=4)
-        for r in range(4):
-            nc.sync.dma_start(ks_window[r:P:SHIFT, :].bitcast(I32), ks_rows[r].bitcast(I32))
         q_raw = [[tile([P, PLACES, HALF], F32, f"q_raw{o}{h}") for h in range(2)] for o in range(2)]
-        for h in range(2):
-            for o in range(2):
-                nc.sync.dma_start(q_raw[o][h][:], q_rows[o][:, :, HALF * h : HALF * (h + 1)])
+
+        def load_queries(o, h):
+            nc.sync.dma_start(q_raw[o][h][:], q_rows[o][:, :, HALF * h : HALF * (h + 1)])
+
+        load_queries(0, 0)
+        load_queries(1, 0)
+        load_queries(0, 1)
 
         q_woven = [tile([P, NQ, PLACES], BF16, f"q_woven{o}") for o in range(2)]
-        q_codes = [tile([P, NQ], U32, name) for name in ("kw_window", "q_codes1")]
+        q_codes = [tile([P, NQ], U32, f"q_codes{o}") for o in range(2)]
         q_scales = [tile([P, NQ], U8, f"q_scales{o}") for o in range(2)]
 
         def weave_queries(o, h, copy):
@@ -98,20 +100,28 @@ def tile_attend_plo_sigb_topk_kernel(tc, qT, k_words, k_scales, vT, ts, kb, us, 
 
         ts_turned = token_columns(ts_window, "ts_listed", "bank10")
         ts_cols = copy_columns(ts_turned, "ts_cols")
-        kb_turned = token_columns(kb_window, "kb_listed", "bank11")
-        weave_queries(0, 0, nc.scalar.copy)
-        kb_cols = copy_columns(kb_turned, "q_raw00")
-        weave_queries(1, 0, nc.scalar.copy)
-        weave_queries(0, 1, nc.scalar.copy)
 
         ks_listed = tile([P, N], U8, "ks_listed")
         nc.vector.tensor_copy(ks_listed[:], ks_window[:].indirect(offsets[:]))
-        k_plane = [tile([P, N], U8, f"k_plane{o}") for o in range(2)]
+        ks_dealt = tile([P, N], U8, "ks_dealt")
         nc.vector.tensor_copy(
-            k_plane[0][:].rearrange("p (t s) -> p s t", t=PLACES),
+            ks_dealt[:].rearrange("p (t s) -> p s t", t=PLACES),
             ks_listed[:].rearrange("p (s t) -> p s t", t=PLACES),
         )
-        nc.sync.dma_start(k_plane[1][0 : P - SHIFT, :].bitcast(I32), k_plane[0][SHIFT:P, :].bitcast(I32))
+        k_planes = tile([P, 2, N], U8, "k_planes")
+        for Q in range(4):
+            nc.sync.dma_start(
+                k_planes[32 * Q : 32 * Q + 4, :, :].bitcast(I32),
+                ks_dealt[KS_ROW + 8 * Q : KS_ROW + 8 * Q + 8, :].bitcast(I32),
+            )
+        load_queries(1, 1)
+
+        kb_turned = token_columns(kb_window, "kb_listed", "bank11")
+        weave_queries(0, 0, nc.scalar.copy)
+        weave_queries(1, 0, nc.scalar.copy)
+        kb_cols = copy_columns(kb_turned, "q_raw10")
+        weave_queries(0, 1, nc.scalar.copy)
+
         us_cols = tile([P, PLACES], F32, "us_cols")
         nc.sync.dma_start(us_cols[:], us[0].rearrange("(p t) z -> p (t z)", t=PLACES))
         v_rows = vT.rearrange("(p j) t -> j p t", j=PLACES)
@@ -119,7 +129,7 @@ def tile_attend_plo_sigb_topk_kernel(tc, qT, k_words, k_scales, vT, ts, kb, us, 
         for j in range(PLACES):
             nc.sync.dma_start(v_window[j][:], v_rows[j])
 
-        kw_listed = tile([P, N], U32, "ks_window")
+        kw_listed = tile([P, N], U32, "kw_listed")
         nc.vector.tensor_copy(kw_listed[:], kw_window[:].bitcast(U32).indirect(offsets[:]))
 
         def key_words(o):
@@ -142,7 +152,7 @@ def tile_attend_plo_sigb_topk_kernel(tc, qT, k_words, k_scales, vT, ts, kb, us, 
                         nc.tensor.matmul_mx(
                             out=score[:, QUARTER * x : QUARTER * (x + 1)],
                             lhsT=words[o][:, 2 * P * t : 2 * P * (t + 1)].bitcast(FP4X4),
-                            lhsT_scale=k_plane[o][:, P * t : P * (t + 1)],
+                            lhsT_scale=k_planes[:, o, P * t : P * (t + 1)],
                             rhs=q_codes[o][:, cols].bitcast(FP8X4),
                             rhs_scale=q_scales[o][:, cols],
                             start=(o == 0),

@@ -54,7 +54,6 @@ def tile_attend_plo_sigb_topk_kernel(tc, qT, k_words, k_scales, vT, ts, kb, us, 
         for cols in (slice(0, T // 2 - 1), slice(T // 2 - 1, T)):
             nc.vector.memset(ts_window[0:LAST, cols].bitcast(I32), 0)
         kb_window = tile([P, T], F32, "kb_window")
-        nc.sync.dma_start(kb_window[LAST:P, :], kb[0:1, :])
         nc.gpsimd.memset(kb_window[0:LAST, :].bitcast(I32), 0)
         warm = tile([P, 2], F32, "warm")
         nc.gpsimd.memset(warm[:, 0:1], 0.0)
@@ -63,14 +62,15 @@ def tile_attend_plo_sigb_topk_kernel(tc, qT, k_words, k_scales, vT, ts, kb, us, 
         make_identity(nc, identity[:])
 
         q_rows = qT[0].rearrange("(o p t) w -> o p t w", o=2, t=PLACES)
-        kw_window = tile([P, T], I32, "kw_window")
-        nc.sync.dma_start(kw_window[:], k_words[0].rearrange("p t b -> p (t b)").bitcast(I32))
         q_raw = [[tile([P, PLACES, HALF], F32, f"q_raw{o}{h}") for h in range(2)] for o in range(2)]
 
         def load_queries(o, h):
             nc.sync.dma_start(q_raw[o][h][:], q_rows[o][:, :, HALF * h : HALF * (h + 1)])
 
         load_queries(0, 0)
+        nc.sync.dma_start(kb_window[LAST:P, :], kb[0:1, :])
+        kw_window = tile([P, T], I32, "kw_window")
+        nc.sync.dma_start(kw_window[:], k_words[0].rearrange("p t b -> p (t b)").bitcast(I32))
         load_queries(1, 0)
         load_queries(0, 1)
 
@@ -99,7 +99,6 @@ def tile_attend_plo_sigb_topk_kernel(tc, qT, k_words, k_scales, vT, ts, kb, us, 
             return columns
 
         ts_turned = token_columns(ts_window, "ts_listed", "bank10")
-        ts_cols = copy_columns(ts_turned, "ts_cols")
 
         ks_listed = tile([P, N], U8, "ks_listed")
         nc.vector.tensor_copy(ks_listed[:], ks_window[:].indirect(offsets[:]))
@@ -109,18 +108,20 @@ def tile_attend_plo_sigb_topk_kernel(tc, qT, k_words, k_scales, vT, ts, kb, us, 
             ks_listed[:].rearrange("p (s t) -> p s t", t=PLACES),
         )
         k_planes = tile([P, 2, N], U8, "k_planes")
-        for Q in range(4):
+        for Q in (0, 2, 1, 3):
             nc.sync.dma_start(
                 k_planes[32 * Q : 32 * Q + 4, :, :].bitcast(I32),
                 ks_dealt[KS_ROW + 8 * Q : KS_ROW + 8 * Q + 8, :].bitcast(I32),
             )
         load_queries(1, 1)
 
-        kb_turned = token_columns(kb_window, "kb_listed", "bank11")
         weave_queries(0, 0, nc.scalar.copy)
+        quantize_queries(0, 0)
+        kb_turned = token_columns(kb_window, "kb_listed", "bank11")
         weave_queries(1, 0, nc.scalar.copy)
-        kb_cols = copy_columns(kb_turned, "q_raw10")
+        ts_cols = copy_columns(ts_turned, "q_raw10")
         weave_queries(0, 1, nc.scalar.copy)
+        kb_cols = copy_columns(kb_turned, "q_raw01")
 
         us_cols = tile([P, PLACES], F32, "us_cols")
         nc.sync.dma_start(us_cols[:], us[0].rearrange("(p t) z -> p (t z)", t=PLACES))
@@ -163,7 +164,6 @@ def tile_attend_plo_sigb_topk_kernel(tc, qT, k_words, k_scales, vT, ts, kb, us, 
                 sig.append(out)
             return sig
 
-        quantize_queries(0, 0)
         quantize_queries(1, 0)
         sig0 = sigmoids(0)
         scaled = [tile([P, PLACES, HALF], BF16, f"scaled{h}") for h in range(2)]
@@ -185,39 +185,41 @@ def tile_attend_plo_sigb_topk_kernel(tc, qT, k_words, k_scales, vT, ts, kb, us, 
                 nc.tensor.transpose(turned[:, u, :], pairs[:, u : N // 2 : 2], identity[:])
             nc.scalar.copy(woven.bitcast(F32), turned[:].rearrange("p u m -> p m u"))
 
-        v_woven01 = tile([P, 2 * P, PLACES], BF16, "v_woven01")
-        v_woven23 = [tile([P, P, PLACES], BF16, f"v_woven{j}") for j in (2, 3)]
+        v_woven = [tile([P, P, PLACES], BF16, f"v_woven{j}") for j in range(PLACES)]
+        v_scales = tile([P, DV], U8, "v_scales")
+        y_scales = tile([P, NQ], U8, "y_scales")
+
+        def quantize_values(j, codes):
+            quantize(nc, codes, v_scales[:, P * j : P * (j + 1)], v_woven[j][:])
 
         for t in range(PLACES - 1):
             nc.vector.tensor_scalar(scaled[0][:, t, :], sig0[t][:], us_cols[:, t : t + 1], None, MULT)
         listed0 = gather_values(0)
-        y_woven = [tile([P, HALF, PLACES], BF16, "v_window0")]
-        weave(nc.vector.tensor_copy, y_woven[0][:], scaled[0][:])
-        y_scales = tile([P, NQ], U8, "y_scales")
-        turn_values(0, listed0, v_woven01[:, 0:P, :])
+        y0_woven = tile([P, HALF, PLACES], BF16, "v_window0")
+        weave(nc.vector.tensor_copy, y0_woven[:], scaled[0][:])
+        turn_values(0, listed0, v_woven[0][:])
         for t in range(PLACES):
             nc.scalar.activation(scaled[1][:, t, :], sig1[t][:], COPY, scale=us_cols[:, t : t + 1])
         listed1 = gather_values(1)
-        y0_codes = tile([P, HALF], U32, "v_window1")
-        quantize(nc, y0_codes[:], y_scales[:, 0:HALF], y_woven[0][:])
-        turn_values(1, listed1, v_woven01[:, P : 2 * P, :])
-        y_woven.append(tile([P, HALF, PLACES], BF16, "v_listed1"))
-        weave(nc.scalar.copy, y_woven[1][:], scaled[1][:])
-        v_scales = tile([P, DV], U8, "v_scales")
+        codes0 = tile([P, HALF + P], U32, "v_window1")
+        quantize(nc, codes0[:, 0:HALF], y_scales[:, 0:HALF], y0_woven[:])
+        quantize_values(0, codes0[:, HALF : HALF + P])
+        turn_values(1, listed1, v_woven[1][:])
+        y1_woven = tile([P, HALF, PLACES], BF16, "v_listed1")
+        weave(nc.scalar.copy, y1_woven[:], scaled[1][:])
         listed2 = gather_values(2)
-        turn_values(2, listed2, v_woven23[0][:])
-        codes = tile([P, HALF + 2 * P], U32, "v_window2")
-        v01_codes = codes[:, HALF : HALF + 2 * P]
-        quantize(nc, v01_codes, v_scales[:, 0 : 2 * P], v_woven01[:])
-        quantize(nc, codes[:, 0:HALF], y_scales[:, HALF:NQ], y_woven[1][:])
-        y_codes = [y0_codes[:], codes[:, 0:HALF]]
+        turn_values(2, listed2, v_woven[2][:])
+        codes1 = tile([P, HALF + P], U32, "v_window2")
+        quantize_values(1, codes1[:, HALF : HALF + P])
+        quantize(nc, codes1[:, 0:HALF], y_scales[:, HALF:NQ], y1_woven[:])
         listed3 = gather_values(3)
-        turn_values(3, listed3, v_woven23[1][:])
+        turn_values(3, listed3, v_woven[3][:])
         v2_codes = tile([P, P], U32, "v_window3")
         v3_codes = tile([P, P], U32, "v3_codes")
-        quantize(nc, v2_codes[:], v_scales[:, 2 * P : 3 * P], v_woven23[0][:])
-        quantize(nc, v3_codes[:], v_scales[:, 3 * P : 4 * P], v_woven23[1][:])
-        v_codes = [v01_codes[:, 0:P], v01_codes[:, P : 2 * P], v2_codes[:], v3_codes[:]]
+        quantize_values(2, v2_codes[:])
+        quantize_values(3, v3_codes[:])
+        y_codes = [codes0[:, 0:HALF], codes1[:, 0:HALF]]
+        v_codes = [codes0[:, HALF : HALF + P], codes1[:, HALF : HALF + P], v2_codes[:], v3_codes[:]]
 
         out_rows = out_0.rearrange("(p j) q -> p j q", j=PLACES)
         result = [tile([P, PLACES, HALF], F32, f"result{h}") for h in range(2)]
@@ -255,7 +257,7 @@ def tile_attend_plo_sigb_topk_kernel(tc, qT, k_words, k_scales, vT, ts, kb, us, 
         o_woven = [tile([P, HALF, PLACES], BF16, f"o_woven{h}") for h in range(2)]
         for h in range(2):
             for x in range(2):
-                copy = nc.scalar.copy if h + x == 2 else nc.vector.tensor_copy
+                copy = nc.scalar.copy if (h, x) == (1, 0) else nc.vector.tensor_copy
                 weave(copy, o_woven[h][:, quarters[x], :], result[h][:, :, quarters[x]])
         for h in range(2):
             cols = slice(HALF * h, HALF * (h + 1))

@@ -21,6 +21,7 @@ N, T, D, NQ, DV = 512, 2048, 1024, 512, 512
 HALF = NQ // 2
 QUARTER = NQ // 4
 LAST = P - 1
+WARM_UPS = 5
 KS_ROW = P - 32
 
 FLOPS = 2 * N * NQ * (D + DV)
@@ -117,6 +118,17 @@ def tile_attend_plo_sigb_topk_kernel(tc, qT, k_words, k_scales, vT, ts, kb, us, 
 
         weave_queries(0, 0, nc.scalar.copy)
         quantize_queries(0, 0)
+        unread = psum.tile([P, 2, HALF], F32, name="bank11")
+        for i in range(WARM_UPS):
+            nc.tensor.matmul_mx(
+                out=unread[:, i % 2, :],
+                lhsT=q_codes[0][:, 0:P].bitcast(FP8X4),
+                lhsT_scale=q_scales[0][:, 0:P],
+                rhs=q_codes[0][:, 0:HALF].bitcast(FP8X4),
+                rhs_scale=q_scales[0][:, 0:HALF],
+                start=True,
+                stop=True,
+            )
         kb_turned = token_columns(kb_window, "kb_listed", "bank11")
         weave_queries(1, 0, nc.scalar.copy)
         ts_cols = copy_columns(ts_turned, "q_raw10")

@@ -41,6 +41,7 @@ def tile_attend_plo_sigb_topk_kernel(tc, qT, k_words, k_scales, vT, ts, kb, us, 
     with ExitStack() as ctx:
         sbuf = ctx.enter_context(tc.tile_pool(name="sbuf", bufs=1))
         psum = ctx.enter_context(tc.psum_pool(name="psum", bufs=1))
+        last = ctx.enter_context(tc.tile_pool(name="last", bufs=1))
 
         def tile(shape, dtype, name):
             return sbuf.tile(shape, dtype, name=name, align_bytes=64)
@@ -56,9 +57,8 @@ def tile_attend_plo_sigb_topk_kernel(tc, qT, k_words, k_scales, vT, ts, kb, us, 
             nc.vector.memset(ts_window[0:LAST, cols].bitcast(I32), 0)
         kb_window = tile([P, T], F32, "kb_window")
         nc.gpsimd.memset(kb_window[0:LAST, :].bitcast(I32), 0)
-        warm = tile([P, 2], F32, "warm")
-        nc.gpsimd.memset(warm[:, 0:1], 0.0)
-        nc.scalar.activation(warm[:, 1:2], warm[:, 0:1], SIGMOID)
+        warm = tile([P, 1], F32, "warm")
+        nc.scalar.activation(warm[0:LAST, :], kb_window[0:LAST, 0:1], SIGMOID)
         identity = tile([P, P], F32, "identity")
         make_identity(nc, identity[:])
 
@@ -138,7 +138,8 @@ def tile_attend_plo_sigb_topk_kernel(tc, qT, k_words, k_scales, vT, ts, kb, us, 
         us_cols = tile([P, PLACES], F32, "us_cols")
         nc.sync.dma_start(us_cols[:], us[0].rearrange("(p t) z -> p (t z)", t=PLACES))
         v_rows = vT.rearrange("(p j) t -> j p t", j=PLACES)
-        v_window = [tile([P, T], F32, f"v_window{j}") for j in range(PLACES)]
+        v_window = [tile([P, T], F32, f"v_window{j}") for j in range(PLACES - 1)]
+        v_window.append(last.tile([P, T], F32, name="v_window3", align_bytes=64, offset=0))
         for j in range(PLACES):
             nc.sync.dma_start(v_window[j][:], v_rows[j])
 
@@ -226,7 +227,7 @@ def tile_attend_plo_sigb_topk_kernel(tc, qT, k_words, k_scales, vT, ts, kb, us, 
         quantize(nc, codes1[:, 0:HALF], y_scales[:, HALF:NQ], y1_woven[:])
         listed3 = gather_values(3)
         turn_values(3, listed3, v_woven[3][:])
-        v2_codes = tile([P, P], U32, "v_window3")
+        v2_codes = last.tile([P, P], U32, name="v2_codes", align_bytes=64, offset=0)
         v3_codes = tile([P, P], U32, "v3_codes")
         quantize_values(2, v2_codes[:])
         quantize_values(3, v3_codes[:])
@@ -253,10 +254,17 @@ def tile_attend_plo_sigb_topk_kernel(tc, qT, k_words, k_scales, vT, ts, kb, us, 
         def store_rows(j0, j1, h):
             nc.sync.dma_start(out_rows[:, j0:j1, HALF * h : HALF * (h + 1)], result[h][:, j0:j1, :])
 
-        for j0, j1 in ((0, 2), (2, 3)):
-            for h in range(2):
-                products(j0, j1, h, slice(0, HALF), f"bank1{j0 + h}")
-                store_rows(j0, j1, h)
+        for h in range(2):
+            products(0, 2, h, slice(0, HALF), f"bank1{h}")
+            store_rows(0, 2, h)
+        o_woven = [
+            last.tile([P, HALF, PLACES], BF16, name="o_woven0", align_bytes=64, offset=4096),
+            tile([P, HALF, PLACES], BF16, "o_woven1"),
+        ]
+        weave(nc.vector.tensor_copy, o_woven[0][:, :, 0:2], result[0][:, 0:2, :])
+        for h in range(2):
+            products(2, 3, h, slice(0, HALF), f"bank1{2 + h}")
+            store_rows(2, 3, h)
         quarters = [slice(QUARTER * x, QUARTER * (x + 1)) for x in range(2)]
         for h in range(2):
             for x in range(2):
@@ -266,11 +274,11 @@ def tile_attend_plo_sigb_topk_kernel(tc, qT, k_words, k_scales, vT, ts, kb, us, 
         out_words = out_1[0].rearrange("p q u -> p (q u)").bitcast(I32)
         o_codes = tile([P, NQ], I32, "o_codes")
         o_scales = tile([P, NQ], U8, "o_scales")
-        o_woven = [tile([P, HALF, PLACES], BF16, f"o_woven{h}") for h in range(2)]
         for h in range(2):
             for x in range(2):
                 copy = nc.scalar.copy if (h, x) == (1, 0) else nc.vector.tensor_copy
-                weave(copy, o_woven[h][:, quarters[x], :], result[h][:, :, quarters[x]])
+                places = slice(2 - 2 * h, PLACES)
+                weave(copy, o_woven[h][:, quarters[x], places], result[h][:, places, quarters[x]])
         for h in range(2):
             cols = slice(HALF * h, HALF * (h + 1))
             quantize(nc, o_codes[:, cols], o_scales[:, cols], o_woven[h][:])

@@ -53,9 +53,10 @@ def tile_attend_plo_sigb_topk_kernel(tc, qT, k_words, k_scales, vT, ts, kb, us, 
         nc.gpsimd.memset(ks_window[0:KS_ROW, :].bitcast(I32), 0)
         ts_window = tile([P, T], F32, "ts_window")
         nc.scalar.dma_start(ts_window[LAST:P, :], ts[0:1, :])
+        kb_window = tile([P, T], F32, "kb_window")
+        nc.scalar.dma_start(kb_window[LAST:P, :], kb[0:1, :])
         for cols in (slice(0, T // 2 - 1), slice(T // 2 - 1, T)):
             nc.vector.memset(ts_window[0:LAST, cols].bitcast(I32), 0)
-        kb_window = tile([P, T], F32, "kb_window")
         nc.gpsimd.memset(kb_window[0:LAST, :].bitcast(I32), 0)
         warm = tile([P, 1], F32, "warm")
         nc.scalar.activation(warm[0:LAST, :], kb_window[0:LAST, 0:1], SIGMOID)
@@ -63,43 +64,23 @@ def tile_attend_plo_sigb_topk_kernel(tc, qT, k_words, k_scales, vT, ts, kb, us, 
         make_identity(nc, identity[:])
 
         q_rows = qT[0].rearrange("(o p t) w -> o p t w", o=2, t=PLACES)
-        q_raw = [[tile([P, PLACES, HALF], F32, f"q_raw{o}{h}") for h in range(2)] for o in range(2)]
-
-        def load_queries(o, h):
-            nc.sync.dma_start(q_raw[o][h][:], q_rows[o][:, :, HALF * h : HALF * (h + 1)])
-
-        load_queries(0, 0)
-        nc.sync.dma_start(kb_window[LAST:P, :], kb[0:1, :])
+        q_raw = [tile([P, PLACES, NQ], F32, f"q_raw{o}") for o in range(2)]
+        nc.sync.dma_start(q_raw[0][:], q_rows[0])
         kw_window = tile([P, T], I32, "kw_window")
         nc.sync.dma_start(kw_window[:], k_words[0].rearrange("p t b -> p (t b)").bitcast(I32))
-        load_queries(1, 0)
-        load_queries(0, 1)
 
-        q_woven = [tile([P, NQ, PLACES], BF16, f"q_woven{o}") for o in range(2)]
+        halves = [slice(HALF * h, HALF * (h + 1)) for h in range(2)]
+        quarters = [slice(QUARTER * x, QUARTER * (x + 1)) for x in range(4)]
         q_codes = [tile([P, NQ], U32, f"q_codes{o}") for o in range(2)]
         q_scales = [tile([P, NQ], U8, f"q_scales{o}") for o in range(2)]
 
-        def weave_queries(o, h, copy):
-            weave(copy, q_woven[o][:, HALF * h : HALF * (h + 1), :], q_raw[o][h][:])
+        def weave_queries(o, cols, copy, name):
+            woven = tile([P, cols.stop - cols.start, PLACES], BF16, name)
+            weave(copy, woven[:], q_raw[o][:, :, cols])
+            return woven
 
-        def quantize_queries(o, h):
-            cols = slice(HALF * h, HALF * (h + 1))
-            quantize(nc, q_codes[o][:, cols], q_scales[o][:, cols], q_woven[o][:, cols, :])
-
-        def token_columns(window, listed_name, bank):
-            listed = tile([P, N], F32, listed_name)
-            nc.vector.tensor_copy(listed[:], window[:].indirect(offsets[:]))
-            turned = psum.tile([P, PLACES, P], F32, name=bank)
-            for t in range(PLACES):
-                nc.tensor.transpose(turned[:, t, :], listed[:, t:N:PLACES], identity[:])
-            return turned
-
-        def copy_columns(turned, name):
-            columns = tile([P, PLACES], F32, name)
-            nc.scalar.copy(columns[:], turned[:, :, LAST])
-            return columns
-
-        ts_turned = token_columns(ts_window, "ts_listed", "bank10")
+        def quantize_queries(o, cols, woven):
+            quantize(nc, q_codes[o][:, cols], q_scales[o][:, cols], woven[:])
 
         ks_listed = tile([P, N], U8, "ks_listed")
         nc.vector.tensor_copy(ks_listed[:], ks_window[:].indirect(offsets[:]))
@@ -114,40 +95,52 @@ def tile_attend_plo_sigb_topk_kernel(tc, qT, k_words, k_scales, vT, ts, kb, us, 
                 k_planes[32 * Q : 32 * Q + 4, :, :].bitcast(I32),
                 ks_dealt[KS_ROW + 8 * Q : KS_ROW + 8 * Q + 8, :].bitcast(I32),
             )
-        load_queries(1, 1)
+        nc.sync.dma_start(q_raw[1][:], q_rows[1])
+        v_rows = vT.rearrange("(p j) t -> j p t", j=PLACES)
 
-        weave_queries(0, 0, nc.scalar.copy)
-        quantize_queries(0, 0)
-        unread = psum.tile([P, 2, HALF], F32, name="bank11")
+        def on_window(j, at, shape, dtype, name):
+            return last.tile(shape, dtype, name=name, align_bytes=64, offset=4 * T * j + at)
+
+        v_window = [on_window(j, 0, [P, T], F32, f"v_window{j}") for j in range(PLACES)]
+        nc.sync.dma_start(v_window[0][:], v_rows[0])
+        us_cols = tile([P, PLACES], F32, "us_cols")
+        nc.sync.dma_start(us_cols[:], us[0].rearrange("(p t) z -> p (t z)", t=PLACES))
+        for j in range(1, PLACES):
+            nc.sync.dma_start(v_window[j][:], v_rows[j])
+
+        def token_columns(window, listed_name, bank):
+            listed = tile([P, N], F32, listed_name)
+            nc.vector.tensor_copy(listed[:], window[:].indirect(offsets[:]))
+            turned = psum.tile([P, PLACES, P], F32, name=bank)
+            for t in range(PLACES):
+                nc.tensor.transpose(turned[:, t, :], listed[:, t:N:PLACES], identity[:])
+            return turned
+
+        ts_turned = token_columns(ts_window, "ts_listed", "bank10")
+        kb_turned = token_columns(kb_window, "kb_listed", "bank11")
+        for h in range(2):
+            quantize_queries(0, halves[h], weave_queries(0, halves[h], nc.scalar.copy, f"q0_woven{h}"))
+        token_cols = tile([P, 2, PLACES], F32, "q_raw0")
+        ts_cols, kb_cols = token_cols[:, 0, :], token_cols[:, 1, :]
+        nc.scalar.copy(ts_cols, ts_turned[:, :, LAST])
+        nc.scalar.copy(kb_cols, kb_turned[:, :, LAST])
+        unread = kb_turned[:].rearrange("p (i t) m -> p i (t m)", i=2)
         for i in range(WARM_UPS):
             nc.tensor.matmul_mx(
                 out=unread[:, i % 2, :],
-                lhsT=q_codes[0][:, 0:P].bitcast(FP8X4),
-                lhsT_scale=q_scales[0][:, 0:P],
-                rhs=q_codes[0][:, 0:HALF].bitcast(FP8X4),
-                rhs_scale=q_scales[0][:, 0:HALF],
+                lhsT=q_codes[0][:, HALF : HALF + P].bitcast(FP8X4),
+                lhsT_scale=q_scales[0][:, HALF : HALF + P],
+                rhs=q_codes[0][:, halves[1]].bitcast(FP8X4),
+                rhs_scale=q_scales[0][:, halves[1]],
                 start=True,
                 stop=True,
             )
-        kb_turned = token_columns(kb_window, "kb_listed", "bank11")
-        weave_queries(1, 0, nc.scalar.copy)
-        ts_cols = copy_columns(ts_turned, "q_raw10")
-        weave_queries(0, 1, nc.scalar.copy)
-        kb_cols = copy_columns(kb_turned, "q_raw01")
-
-        us_cols = tile([P, PLACES], F32, "us_cols")
-        nc.sync.dma_start(us_cols[:], us[0].rearrange("(p t) z -> p (t z)", t=PLACES))
-        v_rows = vT.rearrange("(p j) t -> j p t", j=PLACES)
-        v_window = [tile([P, T], F32, f"v_window{j}") for j in range(PLACES - 1)]
-        v_window.append(last.tile([P, T], F32, name="v_window3", align_bytes=64, offset=0))
-        for j in range(PLACES):
-            nc.sync.dma_start(v_window[j][:], v_rows[j])
 
         kw_listed = tile([P, N], U32, "kw_listed")
         nc.vector.tensor_copy(kw_listed[:], kw_window[:].bitcast(U32).indirect(offsets[:]))
 
         def key_words(o):
-            words = tile([P, 2 * N], U8, f"k_words{o}")
+            words = tile([P, 2 * N], U8, ("kb_listed", "k_words1")[o])
             nc.vector.tensor_copy(
                 words[:].bitcast(U16).rearrange("p (t s) -> p s t", t=PLACES),
                 kw_listed[:].bitcast(U16).rearrange("p (s t o) -> p o s t", t=PLACES, o=2)[:, o],
@@ -156,15 +149,20 @@ def tile_attend_plo_sigb_topk_kernel(tc, qT, k_words, k_scales, vT, ts, kb, us, 
 
         words = [key_words(o) for o in range(2)]
 
+        woven = [weave_queries(1, quarters[x], nc.vector.tensor_copy, f"q1_woven{x}") for x in range(2)]
+        woven.append(weave_queries(1, halves[1], nc.scalar.copy, "kw_listed"))
+        for cols, piece in zip((quarters[0], quarters[1], halves[1]), woven):
+            quantize_queries(1, cols, piece)
+
         def sigmoids(h):
             sig = []
             for t in range(PLACES):
                 score = psum.tile([P, HALF], F32, name=f"bank{h}{t}")
                 for x in range(2):
-                    cols = slice(HALF * h + QUARTER * x, HALF * h + QUARTER * (x + 1))
+                    cols = quarters[2 * h + x]
                     for o in range(2):
                         nc.tensor.matmul_mx(
-                            out=score[:, QUARTER * x : QUARTER * (x + 1)],
+                            out=score[:, quarters[x]],
                             lhsT=words[o][:, 2 * P * t : 2 * P * (t + 1)].bitcast(FP4X4),
                             lhsT_scale=k_planes[:, o, P * t : P * (t + 1)],
                             rhs=q_codes[o][:, cols].bitcast(FP8X4),
@@ -177,14 +175,7 @@ def tile_attend_plo_sigb_topk_kernel(tc, qT, k_words, k_scales, vT, ts, kb, us, 
                 sig.append(out)
             return sig
 
-        quantize_queries(1, 0)
-        sig0 = sigmoids(0)
-        scaled = [tile([P, PLACES, HALF], BF16, f"scaled{h}") for h in range(2)]
-        nc.scalar.activation(scaled[0][:, 3, :], sig0[3][:], COPY, scale=us_cols[:, 3:4])
-        quantize_queries(0, 1)
-        weave_queries(1, 1, nc.vector.tensor_copy)
-        quantize_queries(1, 1)
-        sig1 = sigmoids(1)
+        sig = [sigmoids(h) for h in range(2)]
 
         def gather_values(j):
             listed = tile([P, N], BF16, f"v_listed{j}")
@@ -205,29 +196,31 @@ def tile_attend_plo_sigb_topk_kernel(tc, qT, k_words, k_scales, vT, ts, kb, us, 
         def quantize_values(j, codes):
             quantize(nc, codes, v_scales[:, P * j : P * (j + 1)], v_woven[j][:])
 
-        for t in range(PLACES - 1):
-            nc.vector.tensor_scalar(scaled[0][:, t, :], sig0[t][:], us_cols[:, t : t + 1], None, MULT)
         listed0 = gather_values(0)
-        y0_woven = tile([P, HALF, PLACES], BF16, "v_window0")
-        weave(nc.vector.tensor_copy, y0_woven[:], scaled[0][:])
         turn_values(0, listed0, v_woven[0][:])
+        scaled0 = tile([P, PLACES, HALF], BF16, "scaled0")
         for t in range(PLACES):
-            nc.scalar.activation(scaled[1][:, t, :], sig1[t][:], COPY, scale=us_cols[:, t : t + 1])
+            nc.vector.tensor_scalar(scaled0[:, t, :], sig[0][t][:], us_cols[:, t : t + 1], None, MULT)
+        y0_woven = tile([P, HALF, PLACES], BF16, "y0_woven")
+        weave(nc.vector.tensor_copy, y0_woven[:], scaled0[:])
+        scaled1 = tile([P, PLACES, HALF], BF16, "v_listed0")
+        for t in range(PLACES):
+            nc.scalar.activation(scaled1[:, t, :], sig[1][t][:], COPY, scale=us_cols[:, t : t + 1])
+        y1_woven = tile([P, HALF, PLACES], BF16, "y1_woven")
+        weave(nc.scalar.copy, y1_woven[:], scaled1[:])
         listed1 = gather_values(1)
-        codes0 = tile([P, HALF + P], U32, "v_window1")
-        quantize(nc, codes0[:, 0:HALF], y_scales[:, 0:HALF], y0_woven[:])
+        codes0 = on_window(1, 4096, [P, HALF + P], U32, "codes0")
         quantize_values(0, codes0[:, HALF : HALF + P])
+        quantize(nc, codes0[:, 0:HALF], y_scales[:, 0:HALF], y0_woven[:])
         turn_values(1, listed1, v_woven[1][:])
-        y1_woven = tile([P, HALF, PLACES], BF16, "v_listed1")
-        weave(nc.scalar.copy, y1_woven[:], scaled[1][:])
         listed2 = gather_values(2)
         turn_values(2, listed2, v_woven[2][:])
-        codes1 = tile([P, HALF + P], U32, "v_window2")
+        codes1 = on_window(2, 0, [P, HALF + P], U32, "codes1")
         quantize_values(1, codes1[:, HALF : HALF + P])
         quantize(nc, codes1[:, 0:HALF], y_scales[:, HALF:NQ], y1_woven[:])
         listed3 = gather_values(3)
         turn_values(3, listed3, v_woven[3][:])
-        v2_codes = last.tile([P, P], U32, name="v2_codes", align_bytes=64, offset=0)
+        v2_codes = on_window(3, 0, [P, P], U32, "v2_codes")
         v3_codes = tile([P, P], U32, "v3_codes")
         quantize_values(2, v2_codes[:])
         quantize_values(3, v3_codes[:])
@@ -258,14 +251,13 @@ def tile_attend_plo_sigb_topk_kernel(tc, qT, k_words, k_scales, vT, ts, kb, us, 
             products(0, 2, h, slice(0, HALF), f"bank1{h}")
             store_rows(0, 2, h)
         o_woven = [
-            last.tile([P, HALF, PLACES], BF16, name="o_woven0", align_bytes=64, offset=4096),
+            on_window(3, 4096, [P, HALF, PLACES], BF16, "o_woven0"),
             tile([P, HALF, PLACES], BF16, "o_woven1"),
         ]
         weave(nc.vector.tensor_copy, o_woven[0][:, :, 0:2], result[0][:, 0:2, :])
         for h in range(2):
             products(2, 3, h, slice(0, HALF), f"bank1{2 + h}")
             store_rows(2, 3, h)
-        quarters = [slice(QUARTER * x, QUARTER * (x + 1)) for x in range(2)]
         for h in range(2):
             for x in range(2):
                 products(3, 4, h, quarters[x], f"bank0{2 * h + x}")

@@ -68,6 +68,7 @@ def tile_attend_plo_sigb_topk_kernel(tc, qT, k_words, k_scales, vT, ts, kb, us, 
         nc.sync.dma_start(q_raw[0][:], q_rows[0])
         kw_window = tile([P, T], I32, "kw_window")
         nc.sync.dma_start(kw_window[:], k_words[0].rearrange("p t b -> p (t b)").bitcast(I32))
+        nc.sync.dma_start(q_raw[1][:], q_rows[1])
 
         halves = [slice(HALF * h, HALF * (h + 1)) for h in range(2)]
         quarters = [slice(QUARTER * x, QUARTER * (x + 1)) for x in range(4)]
@@ -95,7 +96,6 @@ def tile_attend_plo_sigb_topk_kernel(tc, qT, k_words, k_scales, vT, ts, kb, us, 
                 k_planes[32 * Q : 32 * Q + 4, :, :].bitcast(I32),
                 ks_dealt[KS_ROW + 8 * Q : KS_ROW + 8 * Q + 8, :].bitcast(I32),
             )
-        nc.sync.dma_start(q_raw[1][:], q_rows[1])
         v_rows = vT.rearrange("(p j) t -> j p t", j=PLACES)
 
         def on_window(j, at, shape, dtype, name):
@@ -124,7 +124,7 @@ def tile_attend_plo_sigb_topk_kernel(tc, qT, k_words, k_scales, vT, ts, kb, us, 
         ts_cols, kb_cols = token_cols[:, 0, :], token_cols[:, 1, :]
         nc.scalar.copy(ts_cols, ts_turned[:, :, LAST])
         nc.scalar.copy(kb_cols, kb_turned[:, :, LAST])
-        unread = kb_turned[:].rearrange("p (i t) m -> p i (t m)", i=2)
+        unread = ts_turned[:].rearrange("p (i t) m -> p i (t m)", i=2)
         for i in range(WARM_UPS):
             nc.tensor.matmul_mx(
                 out=unread[:, i % 2, :],
@@ -140,7 +140,7 @@ def tile_attend_plo_sigb_topk_kernel(tc, qT, k_words, k_scales, vT, ts, kb, us, 
         nc.vector.tensor_copy(kw_listed[:], kw_window[:].bitcast(U32).indirect(offsets[:]))
 
         def key_words(o):
-            words = tile([P, 2 * N], U8, ("kb_listed", "k_words1")[o])
+            words = tile([P, 2 * N], U8, f"k_words{o}")
             nc.vector.tensor_copy(
                 words[:].bitcast(U16).rearrange("p (t s) -> p s t", t=PLACES),
                 kw_listed[:].bitcast(U16).rearrange("p (s t o) -> p o s t", t=PLACES, o=2)[:, o],
@@ -150,7 +150,7 @@ def tile_attend_plo_sigb_topk_kernel(tc, qT, k_words, k_scales, vT, ts, kb, us, 
         words = [key_words(o) for o in range(2)]
 
         woven = [weave_queries(1, quarters[x], nc.vector.tensor_copy, f"q1_woven{x}") for x in range(2)]
-        woven.append(weave_queries(1, halves[1], nc.scalar.copy, "kw_listed"))
+        woven.append(weave_queries(1, halves[1], nc.scalar.copy, "kb_listed"))
         for cols, piece in zip((quarters[0], quarters[1], halves[1]), woven):
             quantize_queries(1, cols, piece)
 

@@ -14,6 +14,7 @@ FP4X4 = mybir.dt.float4_e2m1fn_x4
 SIGMOID = mybir.ActivationFunctionType.Sigmoid
 COPY = mybir.ActivationFunctionType.Copy
 MULT = mybir.AluOpType.mult
+ADD = mybir.AluOpType.add
 
 P = 128
 PLACES = 4
@@ -21,7 +22,7 @@ N, T, D, NQ, DV = 512, 2048, 1024, 512, 512
 HALF = NQ // 2
 QUARTER = NQ // 4
 LAST = P - 1
-WARM_UPS = 5
+WARM_UPS = 6
 KS_ROW = P - 32
 
 FLOPS = 2 * N * NQ * (D + DV)
@@ -48,15 +49,15 @@ def tile_attend_plo_sigb_topk_kernel(tc, qT, k_words, k_scales, vT, ts, kb, us, 
 
         offsets = tile([P, N // 16], U16, "offsets")
         nc.sync.dma_start(offsets[:], offs)
-        ks_window = tile([P, T], U8, "ks_window")
-        nc.sync.dma_start(ks_window[KS_ROW:P, :].bitcast(I32), k_scales.rearrange("o f t -> f o t").bitcast(I32))
-        nc.gpsimd.memset(ks_window[0:KS_ROW, :].bitcast(I32), 0)
         ts_window = tile([P, T], F32, "ts_window")
         nc.scalar.dma_start(ts_window[LAST:P, :], ts[0:1, :])
         kb_window = tile([P, T], F32, "kb_window")
         nc.scalar.dma_start(kb_window[LAST:P, :], kb[0:1, :])
+        ks_window = tile([P, T], U8, "ks_window")
+        nc.sync.dma_start(ks_window[KS_ROW:P, :].bitcast(I32), k_scales.rearrange("o f t -> f o t").bitcast(I32))
         for cols in (slice(0, T // 2 - 1), slice(T // 2 - 1, T)):
             nc.vector.memset(ts_window[0:LAST, cols].bitcast(I32), 0)
+        nc.gpsimd.memset(ks_window[0:KS_ROW, :].bitcast(I32), 0)
         nc.gpsimd.memset(kb_window[0:LAST, :].bitcast(I32), 0)
         warm = tile([P, 1], F32, "warm")
         nc.scalar.activation(warm[0:LAST, :], kb_window[0:LAST, 0:1], SIGMOID)
@@ -72,7 +73,7 @@ def tile_attend_plo_sigb_topk_kernel(tc, qT, k_words, k_scales, vT, ts, kb, us, 
 
         halves = [slice(HALF * h, HALF * (h + 1)) for h in range(2)]
         quarters = [slice(QUARTER * x, QUARTER * (x + 1)) for x in range(4)]
-        q_codes = [tile([P, NQ], U32, f"q_codes{o}") for o in range(2)]
+        q_codes = {}
         q_scales = [tile([P, NQ], U8, f"q_scales{o}") for o in range(2)]
 
         def weave_queries(o, cols, copy, name):
@@ -80,8 +81,24 @@ def tile_attend_plo_sigb_topk_kernel(tc, qT, k_words, k_scales, vT, ts, kb, us, 
             weave(copy, woven[:], q_raw[o][:, :, cols])
             return woven
 
-        def quantize_queries(o, cols, woven):
-            quantize(nc, q_codes[o][:, cols], q_scales[o][:, cols], woven[:])
+        def quantize_queries(o, first, woven, name):
+            count = woven.shape[1] // QUARTER
+            codes = tile([P, count * QUARTER], U32, name)
+            quantize(nc, codes[:], q_scales[o][:, QUARTER * first : QUARTER * (first + count)], woven[:])
+            for x in range(count):
+                q_codes[o, first + x] = codes[:, quarters[x]]
+            return codes
+
+        def token_columns(window, listed_name, bank):
+            listed = tile([P, N], F32, listed_name)
+            nc.vector.tensor_copy(listed[:], window[:].indirect(offsets[:]))
+            turned = psum.tile([P, PLACES, P], F32, name=bank)
+            for t in range(PLACES):
+                nc.tensor.transpose(turned[:, t, :], listed[:, t:N:PLACES], identity[:])
+            return turned
+
+        ts_turned = token_columns(ts_window, "ts_listed", "bank10")
+        kb_turned = token_columns(kb_window, "kb_listed", "bank11")
 
         ks_listed = tile([P, N], U8, "ks_listed")
         nc.vector.tensor_copy(ks_listed[:], ks_window[:].indirect(offsets[:]))
@@ -102,24 +119,13 @@ def tile_attend_plo_sigb_topk_kernel(tc, qT, k_words, k_scales, vT, ts, kb, us, 
             return last.tile(shape, dtype, name=name, align_bytes=64, offset=4 * T * j + at)
 
         v_window = [on_window(j, 0, [P, T], F32, f"v_window{j}") for j in range(PLACES)]
-        nc.sync.dma_start(v_window[0][:], v_rows[0])
         us_cols = tile([P, PLACES], F32, "us_cols")
         nc.sync.dma_start(us_cols[:], us[0].rearrange("(p t) z -> p (t z)", t=PLACES))
-        for j in range(1, PLACES):
+        for j in range(PLACES):
             nc.sync.dma_start(v_window[j][:], v_rows[j])
 
-        def token_columns(window, listed_name, bank):
-            listed = tile([P, N], F32, listed_name)
-            nc.vector.tensor_copy(listed[:], window[:].indirect(offsets[:]))
-            turned = psum.tile([P, PLACES, P], F32, name=bank)
-            for t in range(PLACES):
-                nc.tensor.transpose(turned[:, t, :], listed[:, t:N:PLACES], identity[:])
-            return turned
-
-        ts_turned = token_columns(ts_window, "ts_listed", "bank10")
-        kb_turned = token_columns(kb_window, "kb_listed", "bank11")
-        for h in range(2):
-            quantize_queries(0, halves[h], weave_queries(0, halves[h], nc.scalar.copy, f"q0_woven{h}"))
+        q0_woven = [weave_queries(0, halves[h], nc.scalar.copy, f"q0_woven{h}") for h in range(2)]
+        first_codes = quantize_queries(0, 0, q0_woven[0], "q0_codes0")
         token_cols = tile([P, 2, PLACES], F32, "q_raw0")
         ts_cols, kb_cols = token_cols[:, 0, :], token_cols[:, 1, :]
         nc.scalar.copy(ts_cols, ts_turned[:, :, LAST])
@@ -128,10 +134,10 @@ def tile_attend_plo_sigb_topk_kernel(tc, qT, k_words, k_scales, vT, ts, kb, us, 
         for i in range(WARM_UPS):
             nc.tensor.matmul_mx(
                 out=unread[:, i % 2, :],
-                lhsT=q_codes[0][:, HALF : HALF + P].bitcast(FP8X4),
-                lhsT_scale=q_scales[0][:, HALF : HALF + P],
-                rhs=q_codes[0][:, halves[1]].bitcast(FP8X4),
-                rhs_scale=q_scales[0][:, halves[1]],
+                lhsT=first_codes[:, 0:P].bitcast(FP8X4),
+                lhsT_scale=q_scales[0][:, 0:P],
+                rhs=first_codes[:].bitcast(FP8X4),
+                rhs_scale=q_scales[0][:, halves[0]],
                 start=True,
                 stop=True,
             )
@@ -151,27 +157,33 @@ def tile_attend_plo_sigb_topk_kernel(tc, qT, k_words, k_scales, vT, ts, kb, us, 
 
         woven = [weave_queries(1, quarters[x], nc.vector.tensor_copy, f"q1_woven{x}") for x in range(2)]
         woven.append(weave_queries(1, halves[1], nc.scalar.copy, "kb_listed"))
-        for cols, piece in zip((quarters[0], quarters[1], halves[1]), woven):
-            quantize_queries(1, cols, piece)
+        for x in range(2):
+            quantize_queries(1, x, woven[x], f"q1_codes{x}")
+        quantize_queries(0, 2, q0_woven[1], "q_raw1")
+        quantize_queries(1, 2, woven[2], "q1_codes2")
+
+        def score_pass(score, t, x, o):
+            nc.tensor.matmul_mx(
+                out=score[:, quarters[x % 2]],
+                lhsT=words[o][:, 2 * P * t : 2 * P * (t + 1)].bitcast(FP4X4),
+                lhsT_scale=k_planes[:, o, P * t : P * (t + 1)],
+                rhs=q_codes[o, x].bitcast(FP8X4),
+                rhs_scale=q_scales[o][:, quarters[x]],
+                start=(o == 0),
+                stop=(o == 1),
+            )
 
         def sigmoids(h):
+            scores = [psum.tile([P, HALF], F32, name=f"bank{h}{t}") for t in range(PLACES)]
+            for o in range(2):
+                for t in range(PLACES):
+                    score_pass(scores[t], t, 2 * h, o)
             sig = []
             for t in range(PLACES):
-                score = psum.tile([P, HALF], F32, name=f"bank{h}{t}")
-                for x in range(2):
-                    cols = quarters[2 * h + x]
-                    for o in range(2):
-                        nc.tensor.matmul_mx(
-                            out=score[:, quarters[x]],
-                            lhsT=words[o][:, 2 * P * t : 2 * P * (t + 1)].bitcast(FP4X4),
-                            lhsT_scale=k_planes[:, o, P * t : P * (t + 1)],
-                            rhs=q_codes[o][:, cols].bitcast(FP8X4),
-                            rhs_scale=q_scales[o][:, cols],
-                            start=(o == 0),
-                            stop=(o == 1),
-                        )
+                for o in range(2):
+                    score_pass(scores[t], t, 2 * h + 1, o)
                 out = tile([P, HALF], F32, f"sig{h}{t}")
-                nc.scalar.activation(out[:], score[:], SIGMOID, bias=kb_cols[:, t : t + 1], scale=ts_cols[:, t : t + 1])
+                nc.scalar.activation(out[:], scores[t][:], SIGMOID, bias=kb_cols[:, t : t + 1], scale=ts_cols[:, t : t + 1])
                 sig.append(out)
             return sig
 
@@ -198,20 +210,21 @@ def tile_attend_plo_sigb_topk_kernel(tc, qT, k_words, k_scales, vT, ts, kb, us, 
 
         listed0 = gather_values(0)
         turn_values(0, listed0, v_woven[0][:])
-        scaled0 = tile([P, PLACES, HALF], BF16, "scaled0")
-        for t in range(PLACES):
-            nc.vector.tensor_scalar(scaled0[:, t, :], sig[0][t][:], us_cols[:, t : t + 1], None, MULT)
+        scaled = [tile([P, PLACES, HALF], BF16, "scaled0"), on_window(0, 0, [P, PLACES, HALF], BF16, "scaled1")]
+        for h in range(2):
+            for t in range(PLACES):
+                if (h, t) < (1, 2):
+                    nc.gpsimd.tensor_scalar(scaled[h][:, t, :], sig[h][t][:], us_cols[:, t : t + 1], 0.0, MULT, ADD)
+                else:
+                    nc.vector.tensor_scalar(scaled[h][:, t, :], sig[h][t][:], us_cols[:, t : t + 1], None, MULT)
         y0_woven = tile([P, HALF, PLACES], BF16, "y0_woven")
-        weave(nc.vector.tensor_copy, y0_woven[:], scaled0[:])
-        scaled1 = tile([P, PLACES, HALF], BF16, "v_listed0")
-        for t in range(PLACES):
-            nc.scalar.activation(scaled1[:, t, :], sig[1][t][:], COPY, scale=us_cols[:, t : t + 1])
+        weave(nc.scalar.copy, y0_woven[:], scaled[0][:])
         y1_woven = tile([P, HALF, PLACES], BF16, "y1_woven")
-        weave(nc.scalar.copy, y1_woven[:], scaled1[:])
+        weave(nc.scalar.copy, y1_woven[:], scaled[1][:])
         listed1 = gather_values(1)
         codes0 = on_window(1, 4096, [P, HALF + P], U32, "codes0")
-        quantize_values(0, codes0[:, HALF : HALF + P])
         quantize(nc, codes0[:, 0:HALF], y_scales[:, 0:HALF], y0_woven[:])
+        quantize_values(0, codes0[:, HALF : HALF + P])
         turn_values(1, listed1, v_woven[1][:])
         listed2 = gather_values(2)
         turn_values(2, listed2, v_woven[2][:])

@@ -22,7 +22,7 @@ N, T, D, NQ, DV = 512, 2048, 1024, 512, 512
 HALF = NQ // 2
 QUARTER = NQ // 4
 LAST = P - 1
-WARM_UPS = 6
+WARM_UPS = 5
 KS_ROW = P - 32
 
 FLOPS = 2 * N * NQ * (D + DV)
@@ -191,14 +191,15 @@ def tile_attend_plo_sigb_topk_kernel(tc, qT, k_words, k_scales, vT, ts, kb, us, 
 
         def gather_values(j):
             listed = tile([P, N], BF16, f"v_listed{j}")
-            nc.vector.tensor_copy(listed[:], v_window[j][:].indirect(offsets[:]))
+            sorted_pairs = listed[:].rearrange("p (u w e) -> p w u e", u=2, e=2)
+            nc.vector.tensor_copy(sorted_pairs, v_window[j][:].indirect(offsets[:]))
             return listed
 
         def turn_values(j, listed, woven):
             pairs = listed[:].bitcast(F32)
             turned = psum.tile([P, 2, P], F32, name=f"bank0{j}")
             for u in range(2):
-                nc.tensor.transpose(turned[:, u, :], pairs[:, u : N // 2 : 2], identity[:])
+                nc.tensor.transpose(turned[:, u, :], pairs[:, P * u : P * (u + 1)], identity[:])
             nc.scalar.copy(woven.bitcast(F32), turned[:].rearrange("p u m -> p m u"))
 
         v_woven = [tile([P, P, PLACES], BF16, f"v_woven{j}") for j in range(PLACES)]

@@ -91,10 +91,11 @@ def tile_attend_plo_sigb_topk_kernel(tc, qT, k_words, k_scales, vT, ts, kb, us, 
 
         def token_columns(window, listed_name, bank):
             listed = tile([P, N], F32, listed_name)
-            nc.vector.tensor_copy(listed[:], window[:].indirect(offsets[:]))
+            dealt = listed[:].bitcast(U32).rearrange("p (t s) -> p s t", t=PLACES)
+            nc.vector.tensor_copy(dealt, window[:].bitcast(U32).indirect(offsets[:]))
             turned = psum.tile([P, PLACES, P], F32, name=bank)
             for t in range(PLACES):
-                nc.tensor.transpose(turned[:, t, :], listed[:, t:N:PLACES], identity[:])
+                nc.tensor.transpose(turned[:, t, :], listed[:, P * t : P * (t + 1)], identity[:])
             return turned
 
         ts_turned = token_columns(ts_window, "ts_listed", "bank10")

@@ -105,8 +105,8 @@ def tile_attend_plo_sigb_topk_kernel(tc, qT, k_words, k_scales, vT, ts, kb, us, 
         nc.vector.tensor_copy(ks_listed[:], ks_window[:].indirect(offsets[:]))
         ks_dealt = tile([P, N], U8, "ks_dealt")
         nc.vector.tensor_copy(
-            ks_dealt[:].rearrange("p (t s) -> p s t", t=PLACES),
-            ks_listed[:].rearrange("p (s t) -> p s t", t=PLACES),
+            ks_dealt[:].rearrange("p (t s) -> p t s", t=PLACES),
+            ks_listed[:].rearrange("p (s t) -> p t s", t=PLACES),
         )
         k_planes = tile([P, 2, N], U8, "k_planes")
         for Q in (0, 2, 1, 3):
@@ -144,13 +144,15 @@ def tile_attend_plo_sigb_topk_kernel(tc, qT, k_words, k_scales, vT, ts, kb, us, 
             )
 
         kw_listed = tile([P, N], U32, "kw_listed")
-        nc.vector.tensor_copy(kw_listed[:], kw_window[:].bitcast(U32).indirect(offsets[:]))
+        nc.vector.tensor_copy(
+            kw_listed[:].rearrange("p (t s) -> p s t", t=PLACES), kw_window[:].bitcast(U32).indirect(offsets[:])
+        )
 
         def key_words(o):
             words = tile([P, 2 * N], U8, f"k_words{o}")
             nc.vector.tensor_copy(
-                words[:].bitcast(U16).rearrange("p (t s) -> p s t", t=PLACES),
-                kw_listed[:].bitcast(U16).rearrange("p (s t o) -> p o s t", t=PLACES, o=2)[:, o],
+                words[:].bitcast(U16),
+                kw_listed[:].bitcast(U16).rearrange("p (c o) -> p o c", o=2)[:, o],
             )
             return words
 

from contextlib import ExitStack

import concourse.mybir as mybir
from concourse.masks import make_identity

F32 = mybir.dt.float32
BF16 = mybir.dt.bfloat16
I32 = mybir.dt.int32
U32 = mybir.dt.uint32
U16 = mybir.dt.uint16
U8 = mybir.dt.uint8
FP8X4 = mybir.dt.float8_e4m3fn_x4
FP4X4 = mybir.dt.float4_e2m1fn_x4
SIGMOID = mybir.ActivationFunctionType.Sigmoid
COPY = mybir.ActivationFunctionType.Copy
MULT = mybir.AluOpType.mult
ADD = mybir.AluOpType.add

P = 128
PLACES = 4
N, T, D, NQ, DV = 512, 2048, 1024, 512, 512
HALF = NQ // 2
QUARTER = NQ // 4
LAST = P - 1
WARM_UPS = 5
KS_ROW = P - 32

FLOPS = 2 * N * NQ * (D + DV)
BYTES = 4 * D * NQ + 4 * P * T + 32 * T + 4 * DV * T + 8 * T + 4 * N + 2 * P * (N // 16) + 5 * DV * NQ + 16 * NQ


def weave(copy, dst, src):
    copy(dst.rearrange("p (c i) t -> p c t i", i=4), src.rearrange("p t (c i) -> p c t i", i=4))


def quantize(nc, codes, scales, woven):
    nc.vector.quantize_mx(out=codes.bitcast(FP8X4), scales=scales, in_=woven.rearrange("p w t -> p (w t)"))


def tile_attend_plo_sigb_topk_kernel(tc, qT, k_words, k_scales, vT, ts, kb, us, offs, out_0, out_1, out_2):
    nc = tc.nc
    with ExitStack() as ctx:
        sbuf = ctx.enter_context(tc.tile_pool(name="sbuf", bufs=1))
        psum = ctx.enter_context(tc.psum_pool(name="psum", bufs=1))
        last = ctx.enter_context(tc.tile_pool(name="last", bufs=1))

        def tile(shape, dtype, name):
            return sbuf.tile(shape, dtype, name=name, align_bytes=64)

        offsets = tile([P, N // 16], U16, "offsets")
        nc.sync.dma_start(offsets[:], offs)
        ts_window = tile([P, T], F32, "ts_window")
        nc.scalar.dma_start(ts_window[LAST:P, :], ts[0:1, :])
        kb_window = tile([P, T], F32, "kb_window")
        nc.scalar.dma_start(kb_window[LAST:P, :], kb[0:1, :])
        ks_window = tile([P, T], U8, "ks_window")
        nc.sync.dma_start(ks_window[KS_ROW:P, :].bitcast(I32), k_scales.rearrange("o f t -> f o t").bitcast(I32))
        for cols in (slice(0, T // 2 - 1), slice(T // 2 - 1, T)):
            nc.vector.memset(ts_window[0:LAST, cols].bitcast(I32), 0)
        nc.gpsimd.memset(ks_window[0:KS_ROW, :].bitcast(I32), 0)
        nc.gpsimd.memset(kb_window[0:LAST, :].bitcast(I32), 0)
        warm = tile([P, 1], F32, "warm")
        nc.scalar.activation(warm[0:LAST, :], kb_window[0:LAST, 0:1], SIGMOID)
        identity = tile([P, P], F32, "identity")
        make_identity(nc, identity[:])

        q_rows = qT[0].rearrange("(o p t) w -> o p t w", o=2, t=PLACES)
        q_raw = [tile([P, PLACES, NQ], F32, f"q_raw{o}") for o in range(2)]
        nc.sync.dma_start(q_raw[0][:], q_rows[0])
        kw_window = tile([P, T], I32, "kw_window")
        nc.sync.dma_start(kw_window[:], k_words[0].rearrange("p t b -> p (t b)").bitcast(I32))
        nc.sync.dma_start(q_raw[1][:], q_rows[1])

        halves = [slice(HALF * h, HALF * (h + 1)) for h in range(2)]
        quarters = [slice(QUARTER * x, QUARTER * (x + 1)) for x in range(4)]
        q_codes = {}
        q_scales = [tile([P, NQ], U8, f"q_scales{o}") for o in range(2)]

        def weave_queries(o, cols, copy, name):
            woven = tile([P, cols.stop - cols.start, PLACES], BF16, name)
            weave(copy, woven[:], q_raw[o][:, :, cols])
            return woven

        def quantize_queries(o, first, woven, name):
            count = woven.shape[1] // QUARTER
            codes = tile([P, count * QUARTER], U32, name)
            quantize(nc, codes[:], q_scales[o][:, QUARTER * first : QUARTER * (first + count)], woven[:])
            for x in range(count):
                q_codes[o, first + x] = codes[:, quarters[x]]
            return codes

        def token_columns(window, listed_name, bank):
            listed = tile([P, N], F32, listed_name)
            dealt = listed[:].bitcast(U32).rearrange("p (t s) -> p s t", t=PLACES)
            nc.vector.tensor_copy(dealt, window[:].bitcast(U32).indirect(offsets[:]))
            turned = psum.tile([P, PLACES, P], F32, name=bank)
            for t in range(PLACES):
                nc.tensor.transpose(turned[:, t, :], listed[:, P * t : P * (t + 1)], identity[:])
            return turned

        ts_turned = token_columns(ts_window, "ts_listed", "bank10")
        kb_turned = token_columns(kb_window, "kb_listed", "bank11")

        ks_listed = tile([P, N], U8, "ks_listed")
        nc.vector.tensor_copy(ks_listed[:], ks_window[:].indirect(offsets[:]))
        ks_dealt = tile([P, N], U8, "ks_dealt")
        nc.vector.tensor_copy(
            ks_dealt[:].rearrange("p (t s) -> p t s", t=PLACES),
            ks_listed[:].rearrange("p (s t) -> p t s", t=PLACES),
        )
        k_planes = tile([P, 2, N], U8, "k_planes")
        for Q in (0, 2, 1, 3):
            nc.sync.dma_start(
                k_planes[32 * Q : 32 * Q + 4, :, :].bitcast(I32),
                ks_dealt[KS_ROW + 8 * Q : KS_ROW + 8 * Q + 8, :].bitcast(I32),
            )
        v_rows = vT.rearrange("(p j) t -> j p t", j=PLACES)

        def on_window(j, at, shape, dtype, name):
            return last.tile(shape, dtype, name=name, align_bytes=64, offset=4 * T * j + at)

        v_window = [on_window(j, 0, [P, T], F32, f"v_window{j}") for j in range(PLACES)]
        us_cols = tile([P, PLACES], F32, "us_cols")
        nc.sync.dma_start(us_cols[:], us[0].rearrange("(p t) z -> p (t z)", t=PLACES))
        for j in range(PLACES):
            nc.sync.dma_start(v_window[j][:], v_rows[j])

        q0_woven = [weave_queries(0, halves[h], nc.scalar.copy, f"q0_woven{h}") for h in range(2)]
        first_codes = quantize_queries(0, 0, q0_woven[0], "q0_codes0")
        token_cols = tile([P, 2, PLACES], F32, "q_raw0")
        ts_cols, kb_cols = token_cols[:, 0, :], token_cols[:, 1, :]
        nc.scalar.copy(ts_cols, ts_turned[:, :, LAST])
        nc.scalar.copy(kb_cols, kb_turned[:, :, LAST])
        unread = ts_turned[:].rearrange("p (i t) m -> p i (t m)", i=2)
        for i in range(WARM_UPS):
            nc.tensor.matmul_mx(
                out=unread[:, i % 2, :],
                lhsT=first_codes[:, 0:P].bitcast(FP8X4),
                lhsT_scale=q_scales[0][:, 0:P],
                rhs=first_codes[:].bitcast(FP8X4),
                rhs_scale=q_scales[0][:, halves[0]],
                start=True,
                stop=True,
            )

        kw_listed = tile([P, N], U32, "kw_listed")
        nc.vector.tensor_copy(
            kw_listed[:].rearrange("p (t s) -> p s t", t=PLACES), kw_window[:].bitcast(U32).indirect(offsets[:])
        )

        def key_words(o):
            words = tile([P, 2 * N], U8, f"k_words{o}")
            nc.vector.tensor_copy(
                words[:].bitcast(U16),
                kw_listed[:].bitcast(U16).rearrange("p (c o) -> p o c", o=2)[:, o],
            )
            return words

        words = [key_words(o) for o in range(2)]

        woven = [weave_queries(1, quarters[x], nc.vector.tensor_copy, f"q1_woven{x}") for x in range(2)]
        woven.append(weave_queries(1, halves[1], nc.scalar.copy, "kb_listed"))
        for x in range(2):
            quantize_queries(1, x, woven[x], f"q1_codes{x}")
        quantize_queries(0, 2, q0_woven[1], "q_raw1")
        quantize_queries(1, 2, woven[2], "q1_codes2")

        def score_pass(score, t, x, o):
            nc.tensor.matmul_mx(
                out=score[:, quarters[x % 2]],
                lhsT=words[o][:, 2 * P * t : 2 * P * (t + 1)].bitcast(FP4X4),
                lhsT_scale=k_planes[:, o, P * t : P * (t + 1)],
                rhs=q_codes[o, x].bitcast(FP8X4),
                rhs_scale=q_scales[o][:, quarters[x]],
                start=(o == 0),
                stop=(o == 1),
            )

        def sigmoids(h):
            scores = [psum.tile([P, HALF], F32, name=f"bank{h}{t}") for t in range(PLACES)]
            for o in range(2):
                for t in range(PLACES):
                    score_pass(scores[t], t, 2 * h, o)
            sig = []
            for t in range(PLACES):
                for o in range(2):
                    score_pass(scores[t], t, 2 * h + 1, o)
                out = tile([P, HALF], F32, f"sig{h}{t}")
                nc.scalar.activation(out[:], scores[t][:], SIGMOID, bias=kb_cols[:, t : t + 1], scale=ts_cols[:, t : t + 1])
                sig.append(out)
            return sig

        sig = [sigmoids(h) for h in range(2)]

        def gather_values(j):
            listed = tile([P, N], BF16, f"v_listed{j}")
            sorted_pairs = listed[:].rearrange("p (u w e) -> p w u e", u=2, e=2)
            nc.vector.tensor_copy(sorted_pairs, v_window[j][:].indirect(offsets[:]))
            return listed

        def turn_values(j, listed, woven):
            pairs = listed[:].bitcast(F32)
            turned = psum.tile([P, 2, P], F32, name=f"bank0{j}")
            for u in range(2):
                nc.tensor.transpose(turned[:, u, :], pairs[:, P * u : P * (u + 1)], identity[:])
            nc.scalar.copy(woven.bitcast(F32), turned[:].rearrange("p u m -> p m u"))

        v_woven = [tile([P, P, PLACES], BF16, f"v_woven{j}") for j in range(PLACES)]
        v_scales = tile([P, DV], U8, "v_scales")
        y_scales = tile([P, NQ], U8, "y_scales")

        def quantize_values(j, codes):
            quantize(nc, codes, v_scales[:, P * j : P * (j + 1)], v_woven[j][:])

        listed0 = gather_values(0)
        turn_values(0, listed0, v_woven[0][:])
        scaled = [tile([P, PLACES, HALF], BF16, "scaled0"), on_window(0, 0, [P, PLACES, HALF], BF16, "scaled1")]
        for h in range(2):
            for t in range(PLACES):
                if (h, t) < (1, 2):
                    nc.gpsimd.tensor_scalar(scaled[h][:, t, :], sig[h][t][:], us_cols[:, t : t + 1], 0.0, MULT, ADD)
                else:
                    nc.vector.tensor_scalar(scaled[h][:, t, :], sig[h][t][:], us_cols[:, t : t + 1], None, MULT)
        y0_woven = tile([P, HALF, PLACES], BF16, "y0_woven")
        weave(nc.scalar.copy, y0_woven[:], scaled[0][:])
        y1_woven = tile([P, HALF, PLACES], BF16, "y1_woven")
        weave(nc.scalar.copy, y1_woven[:], scaled[1][:])
        listed1 = gather_values(1)
        codes0 = on_window(1, 4096, [P, HALF + P], U32, "codes0")
        quantize(nc, codes0[:, 0:HALF], y_scales[:, 0:HALF], y0_woven[:])
        quantize_values(0, codes0[:, HALF : HALF + P])
        turn_values(1, listed1, v_woven[1][:])
        listed2 = gather_values(2)
        turn_values(2, listed2, v_woven[2][:])
        codes1 = on_window(2, 0, [P, HALF + P], U32, "codes1")
        quantize_values(1, codes1[:, HALF : HALF + P])
        quantize(nc, codes1[:, 0:HALF], y_scales[:, HALF:NQ], y1_woven[:])
        listed3 = gather_values(3)
        turn_values(3, listed3, v_woven[3][:])
        v2_codes = on_window(3, 0, [P, P], U32, "v2_codes")
        v3_codes = tile([P, P], U32, "v3_codes")
        quantize_values(2, v2_codes[:])
        quantize_values(3, v3_codes[:])
        y_codes = [codes0[:, 0:HALF], codes1[:, 0:HALF]]
        v_codes = [codes0[:, HALF : HALF + P], codes1[:, HALF : HALF + P], v2_codes[:], v3_codes[:]]

        out_rows = out_0.rearrange("(p j) q -> p j q", j=PLACES)
        result = [tile([P, PLACES, HALF], F32, f"result{h}") for h in range(2)]

        def products(j0, j1, h, cols, bank):
            acc = psum.tile([P, j1 - j0, cols.stop - cols.start], F32, name=bank)
            for j in range(j0, j1):
                nc.tensor.matmul_mx(
                    out=acc[:, j - j0, :],
                    lhsT=v_codes[j].bitcast(FP8X4),
                    lhsT_scale=v_scales[:, P * j : P * (j + 1)],
                    rhs=y_codes[h][:, cols].bitcast(FP8X4),
                    rhs_scale=y_scales[:, HALF * h + cols.start : HALF * h + cols.stop],
                    start=True,
                    stop=True,
                )
            nc.scalar.copy(result[h][:, j0:j1, cols], acc[:])

        def store_rows(j0, j1, h):
            nc.sync.dma_start(out_rows[:, j0:j1, HALF * h : HALF * (h + 1)], result[h][:, j0:j1, :])

        for h in range(2):
            products(0, 2, h, slice(0, HALF), f"bank1{h}")
            store_rows(0, 2, h)
        o_woven = [
            on_window(3, 4096, [P, HALF, PLACES], BF16, "o_woven0"),
            tile([P, HALF, PLACES], BF16, "o_woven1"),
        ]
        weave(nc.vector.tensor_copy, o_woven[0][:, :, 0:2], result[0][:, 0:2, :])
        for h in range(2):
            products(2, 3, h, slice(0, HALF), f"bank1{2 + h}")
            store_rows(2, 3, h)
        for h in range(2):
            for x in range(2):
                products(3, 4, h, quarters[x], f"bank0{2 * h + x}")
            store_rows(3, 4, h)

        out_words = out_1[0].rearrange("p q u -> p (q u)").bitcast(I32)
        o_codes = tile([P, NQ], I32, "o_codes")
        o_scales = tile([P, NQ], U8, "o_scales")
        for h in range(2):
            for x in range(2):
                copy = nc.scalar.copy if (h, x) == (1, 0) else nc.vector.tensor_copy
                places = slice(2 - 2 * h, PLACES)
                weave(copy, o_woven[h][:, quarters[x], places], result[h][:, places, quarters[x]])
        for h in range(2):
            cols = slice(HALF * h, HALF * (h + 1))
            quantize(nc, o_codes[:, cols], o_scales[:, cols], o_woven[h][:])
            nc.sync.dma_start(out_words[:, cols], o_codes[:, cols])
        for Q in range(4):
            (nc.scalar, nc.sync)[Q % 2].dma_start(
                out_2[0, 4 * Q : 4 * Q + 4, :].bitcast(I32), o_scales[32 * Q : 32 * Q + 4, :].bitcast(I32)
            )
